import numpy as np
import ml_dtypes


def mxq(x, axis, fmt="e4m3"):
    dtype, down = {"e4m3": (ml_dtypes.float8_e4m3fn, 7), "e5m2": (ml_dtypes.float8_e5m2, 14)}[fmt]
    v = np.moveaxis(np.asarray(x, np.float32).astype(ml_dtypes.bfloat16).astype(np.float64), axis, -1)
    blocks = v.reshape(v.shape[:-1] + (-1, 32))
    amax = np.abs(blocks).max(-1, keepdims=True)
    byte = np.maximum(np.where(amax > 0, np.frexp(amax)[1] - 1 + 127, 0) - down, 1)
    scale = np.exp2(byte - 127.0)
    codes = (blocks / scale).astype(np.float32).astype(dtype).astype(np.float64)
    return np.moveaxis((codes * scale).reshape(v.shape), -1, axis)


WIDE = False


def mx_kscale(k):
    if not WIDE:
        return np.ones(k)
    levels = np.array([10, -10, 5, -5, 0])
    if k % 512:
        return np.exp2(np.random.permutation(np.resize(levels, k // 32))).repeat(32)
    a = np.empty((k // 512, 16))
    for p in range(k // 512):
        a[p, :8] = np.random.permutation(np.resize(levels, 8))
        for g in range(8):
            far = levels[np.abs(levels - a[p, g]) >= 10]
            a[p, g + 8] = far[np.random.randint(len(far))]
    return np.exp2(a.ravel()).repeat(32)


def f64(x):
    return np.asarray(x).astype(np.float64)


def striped(idx):
    return np.tile(idx.reshape(-1, 16).T, (8, 1)).astype(np.uint16)


def unstriped(offs):
    return offs[:16].T.reshape(-1).astype(np.int64)


E2M1 = np.array([0.0, 0.5, 1.0, 1.5, 2.0, 3.0, 4.0, 6.0, -0.0, -0.5, -1.0, -1.5, -2.0, -3.0, -4.0, -6.0])


def pack_weight(w, fmt):
    k, n = w.shape
    w = f64(np.asarray(w, np.float32).astype(ml_dtypes.bfloat16)).reshape(k // 32, 32, n)
    amax = np.abs(w).max(1)
    if fmt == "e4m3":
        byte = np.frexp(amax)[1] - 1 + 127 - 7
    else:
        mant, ex = np.frexp(amax / 6.0)
        byte = np.where(mant > 0.5, ex, ex - 1) + 127
    byte = np.clip(np.where(amax > 0, byte, 1), 1, 254)
    scaled = (w * np.exp2(127.0 - byte)[:, None, :]).reshape(k, n).astype(np.float32)
    by_word = np.ascontiguousarray(scaled.reshape(k // 512, 128, 4, n).transpose(0, 1, 3, 2))
    if fmt == "e4m3":
        words = by_word.astype(ml_dtypes.float8_e4m3fn).view(np.uint8)
    else:
        c = by_word.astype(ml_dtypes.float4_e2m1fn).view(np.uint8) & 0xF
        words = (c[..., 0::2] | (c[..., 1::2] << 4)).reshape(k // 512, 128, 2 * n)
    return np.ascontiguousarray(words), np.ascontiguousarray(byte.astype(np.uint8).reshape(k // 512, 16, n))


def unpack_weight(words, scales, fmt):
    g, _, n = scales.shape
    words = np.ascontiguousarray(words).reshape(g, 128, n, -1)
    if fmt == "e4m3":
        vals = words.view(ml_dtypes.float8_e4m3fn).astype(np.float64)
    else:
        nib = np.empty((g, 128, n, 4), np.uint8)
        nib[..., 0::2] = words & 0xF
        nib[..., 1::2] = words >> 4
        vals = E2M1[nib]
    vals = vals * np.repeat(np.exp2(scales.astype(np.float64) - 127.0), 8, axis=1)[..., None]
    return vals.transpose(0, 1, 3, 2).reshape(g * 512, n)


def gelu(v):
    return 0.5 * v * (1.0 + np.tanh(np.sqrt(2.0 / np.pi) * (v + 0.044715 * v**3)))


K, H, T, S, T3, S2, P = 512, 1024, 2048, 1024, 1024, 512, 512

def setup_inputs():
    n = np.random.standard_normal
    s = mx_kscale(K)[:, None]
    u = mx_kscale(H)[:, None]
    d = {}
    d["tab_words"], d["tab_scales"] = pack_weight(n((K, T)) * s, "e4m3")
    d["tab2_words"], d["tab2_scales"] = pack_weight(n((H, T3)) / u / H ** 0.5, "e4m3")
    d["wa"] = (1.5 * n((K, H)) / s / K ** 0.5).astype(np.float32)
    d["wb_words"], d["wb_scales"] = pack_weight(1.5 * n((K, H)) / s / K ** 0.5, "e2m1")
    d["w3"] = (n((K, H)) / s * u.T / K ** 0.5).astype(np.float32)
    d["leaf"] = (0.8 * n((S2, P))).astype(np.float32)
    d["panel"] = (0.8 * n(S2)).astype(np.float32)
    d["offs"] = striped(np.random.permutation(T)[:S])
    d["offs2"] = striped(np.random.permutation(T3)[:S2])
    d["pos1"] = striped(np.random.permutation(S)[:P])
    d["pos2"] = striped(np.random.permutation(S)[:P])
    return d

def reference(tab_words, tab_scales, tab2_words, tab2_scales, wa, wb_words, wb_scales, w3, leaf, panel, offs, offs2, pos1, pos2):
    v = unpack_weight(tab_words, tab_scales, "e4m3")[:, unstriped(offs)]
    v2 = unpack_weight(tab2_words, tab2_scales, "e4m3")[:, unstriped(offs2)]
    wb = unpack_weight(wb_words, wb_scales, "e2m1")
    fa = mxq(f64(wa), 0, "e4m3").T @ v
    fb = wb.T @ v
    f3 = mxq(f64(w3), 0, "e4m3").T @ v
    h = (np.tanh(fa) - np.tanh(fb)) * f3
    e = v2.T @ mxq(h, 0, "e4m3")
    left = e[:, unstriped(pos1)] + f64(leaf)
    right = e[:, unstriped(pos2)] + f64(panel)[:, None]
    return left * right

@@ -1,0 +1,270 @@
+from contextlib import ExitStack
+
+import concourse.mybir as mybir
+
+K, H, T, S, T3, S2, NP = 512, 1024, 2048, 1024, 1024, 512, 512
+FLOPS = 2 * K * H * S * 3 + 2 * H * S2 * S
+
+F32 = mybir.dt.float32
+BF16 = mybir.dt.bfloat16
+I32 = mybir.dt.int32
+U32 = mybir.dt.uint32
+U16 = mybir.dt.uint16
+U8 = mybir.dt.uint8
+FP8X4 = mybir.dt.float8_e4m3fn_x4
+FP4X4 = mybir.dt.float4_e2m1fn_x4
+ADD = mybir.AluOpType.add
+SUB = mybir.AluOpType.subtract
+MULT = mybir.AluOpType.mult
+TANH = mybir.ActivationFunctionType.Tanh
+
+P = 128
+UNITS = 16
+VECTOR_SUBS = (3, 7, 11, 15)
+
+
+def tile_list_bookmatch_leaf_scores_kernel(
+    tc, tab_words, tab_scales, tab2_words, tab2_scales, wa, wb_words, wb_scales, w3, leaf, panel, offs, offs2, pos1, pos2, out
+):
+    nc = tc.nc
+    with ExitStack() as ctx:
+        lists = ctx.enter_context(tc.tile_pool(name="lists", bufs=1))
+        keep = ctx.enter_context(tc.tile_pool(name="keep", bufs=1))
+        work = ctx.enter_context(tc.tile_pool(name="work", bufs=1))
+        psum = ctx.enter_context(tc.psum_pool(name="psum", bufs=1))
+
+        offs_t = lists.tile([P, S // 16], U16, name="offs_t")
+        offs2_t = lists.tile([P, S2 // 16], U16, name="offs2_t")
+        pos1_t = lists.tile([P, NP // 16], U16, name="pos1_t")
+        pos2_t = lists.tile([P, NP // 16], U16, name="pos2_t")
+
+        tab_w = keep.tile([P, T], I32, name="tab_w", align_bytes=64)
+        tab_s = keep.tile([P, T], U8, name="tab_s", align_bytes=64)
+        tab2_w = [keep.tile([P, T3], I32, name=f"tab2_w{b}", align_bytes=64) for b in range(2)]
+        tab2_s = keep.tile([P, T3], U8, name="tab2_s", align_bytes=64)
+        wb_raw = keep.tile([P, 2 * H], U8, name="wb_raw", align_bytes=64)
+        wb_raw_s = keep.tile([P, H], U8, name="wb_raw_s", align_bytes=64)
+        wa_head = [keep.tile([P, 4, 256], F32, name=f"wa_head{half}", align_bytes=64) for half in range(2)]
+        wa_raw = keep.tile([P, 4, 512], F32, name="wa_raw", align_bytes=64)
+        w3_raw = [keep.tile([P, 4, 512], F32, name=f"w3_raw{b}", align_bytes=64) for b in range(2)]
+        leaf_t = keep.tile([P, 4, NP], F32, name="leaf_t", align_bytes=64)
+        panel_t = keep.tile([P, 4], F32, name="panel_t", align_bytes=64)
+        warm = keep.tile([P, 1], F32, name="warm")
+        warm_out = keep.tile([P, 1], F32, name="warm_out")
+
+        nc.gpsimd.memset(tab_s[:].bitcast(I32), 0)
+        nc.vector.memset(wb_raw_s[:].bitcast(I32), 0)
+        nc.vector.memset(tab2_s[:].bitcast(I32), 0)
+        nc.vector.memset(warm[:], 0.0)
+        nc.scalar.activation(warm_out[:], warm[:], TANH)
+
+        wa_rows = wa.rearrange("(p j) c -> p j c", j=4)
+        w3_rows = w3.rearrange("(p j) c -> p j c", j=4)
+        nc.sync.dma_start(offs_t[:], offs)
+        nc.sync.dma_start(tab_w[:], tab_words[0].rearrange("p t i -> p (t i)").bitcast(I32))
+        for q in range(4):
+            nc.sync.dma_start(tab_s[32 * q : 32 * q + 4, :].bitcast(I32), tab_scales[0, 4 * q : 4 * q + 4, :].bitcast(I32))
+        for half in range(2):
+            nc.sync.dma_start(wa_head[half][:], wa_rows[:, :, 256 * half : 256 * (half + 1)])
+        nc.sync.dma_start(wb_raw[:].bitcast(I32), wb_words[0].bitcast(I32))
+        for q in range(4):
+            nc.sync.dma_start(wb_raw_s[32 * q : 32 * q + 4, :].bitcast(I32), wb_scales[0, 4 * q : 4 * q + 4, :].bitcast(I32))
+        nc.sync.dma_start(w3_raw[0][:], w3_rows[:, :, 0:512])
+        nc.sync.dma_start(wa_raw[:], wa_rows[:, :, 512:1024])
+        nc.sync.dma_start(w3_raw[1][:], w3_rows[:, :, 512:1024])
+        nc.sync.dma_start(offs2_t[:], offs2)
+        for b in range(2):
+            nc.sync.dma_start(tab2_w[b][:], tab2_words[b].rearrange("p t i -> p (t i)").bitcast(I32))
+        for q in range(4):
+            nc.sync.dma_start(tab2_s[32 * q : 32 * q + 8, :].bitcast(I32), tab2_scales[:, 4 * q : 4 * q + 4, :].bitcast(I32))
+        nc.sync.dma_start(pos1_t[:], pos1)
+        nc.sync.dma_start(pos2_t[:], pos2)
+        with nc.allow_non_contiguous_dma(reason="one panel value a partition"):
+            nc.sync.dma_start(panel_t[:], panel.rearrange("(m p) -> p m", p=P))
+        nc.sync.dma_start(leaf_t[:], leaf.rearrange("(m p) n -> p m n", p=P))
+
+        v_w = keep.tile([P, S], U32, name="v_w", align_bytes=64)
+        v_s = keep.tile([P, S], U8, name="v_s", align_bytes=64)
+        v2_w = [keep.tile([P, S2], U32, name=f"v2_w{b}", align_bytes=64) for b in range(2)]
+        v2_s = keep.tile([P, S2], U8, name="v2_s", align_bytes=64)
+        wb_w = [keep.tile([P, 1024], U8, name=f"wb_w{b}", align_bytes=64) for b in range(2)]
+        wb_s = [keep.tile([P, 512], U8, name=f"wb_s{b}", align_bytes=64) for b in range(2)]
+        wa_bf = [keep.tile([P, 2048], BF16, name=f"wa_bf{b}", align_bytes=64) for b in range(2)]
+        w3_bf = [keep.tile([P, 2048], BF16, name=f"w3_bf{b}", align_bytes=64) for b in range(2)]
+        wa_w = [keep.tile([P, 512], U32, name=f"wa_w{b}", align_bytes=64) for b in range(2)]
+        wa_s = [keep.tile([P, 512], U8, name=f"wa_s{b}", align_bytes=64) for b in range(2)]
+        w3_w = [keep.tile([P, 512], U32, name=f"w3_w{b}", align_bytes=64) for b in range(2)]
+        w3_s = [keep.tile([P, 512], U8, name=f"w3_s{b}", align_bytes=64) for b in range(2)]
+        h_bf = [keep.tile([P, 4 * S], BF16, name=f"h_bf{b}", align_bytes=64) for b in range(2)]
+        h_w = [keep.tile([P, S], U32, name=f"h_w{b}", align_bytes=64) for b in range(2)]
+        h_s = [keep.tile([P, S], U8, name=f"h_s{b}", align_bytes=64) for b in range(2)]
+        e_t = [keep.tile([P, S], F32, name=f"e{m}", align_bytes=64) for m in range(4)]
+
+        def gather_v(lo, hi):
+            picks = offs_t[:, lo // 16 : hi // 16]
+            nc.vector.tensor_copy(v_w[:, lo:hi], tab_w[:].bitcast(U32).indirect(picks))
+            nc.vector.tensor_copy(v_s[:, lo:hi], tab_s[:].indirect(picks))
+
+        def gather_v2(lo, hi):
+            picks = offs2_t[:, lo // 16 : hi // 16]
+            for b in range(2):
+                nc.vector.tensor_copy(v2_w[b][:, lo:hi], tab2_w[b][:].bitcast(U32).indirect(picks))
+            nc.vector.tensor_copy(v2_s[:, lo:hi], tab2_s[:].indirect(picks))
+
+        def deal_wb(b):
+            nc.vector.tensor_copy(
+                wb_w[b][:].bitcast(U16).rearrange("p (t q) -> p t q", t=4),
+                wb_raw[:, 1024 * b : 1024 * (b + 1)].bitcast(U16).rearrange("p (q t) -> p t q", t=4),
+            )
+            nc.vector.tensor_copy(
+                wb_s[b][:].rearrange("p (t q) -> p t q", t=4),
+                wb_raw_s[:, 512 * b : 512 * (b + 1)].rearrange("p (q t) -> p t q", t=4),
+            )
+
+        def round_weight(copy, bf, raw, q0):
+            count = raw.shape[2] // 4
+            copy(bf[:].rearrange("p (t q i) -> p q t i", t=4, i=4)[:, q0 : q0 + count], raw[:].rearrange("p i (q t) -> p q t i", t=4))
+
+        def quantize(words, scales, bf):
+            nc.vector.quantize_mx(out=words.bitcast(FP8X4), scales=scales, in_=bf)
+
+        def product(bank, u, weight, weight_scale):
+            cols = slice(P * (u % 8), P * (u % 8 + 1))
+            for t in range(4):
+                nc.tensor.matmul_mx(
+                    out=bank[:, P * t : P * (t + 1)],
+                    lhsT=weight(t),
+                    lhsT_scale=weight_scale[:, P * t : P * (t + 1)],
+                    rhs=v_w[:, cols].bitcast(FP8X4),
+                    rhs_scale=v_s[:, cols],
+                    start=True,
+                    stop=True,
+                )
+
+        def woven(bank):
+            return bank[:].rearrange("p (t j) -> p j t", t=4)
+
+        def by_four(ap):
+            return ap.rearrange("p (j t) -> p j t", t=4)
+
+        tanh_a, tanh_b, diff, f3 = {}, {}, {}, {}
+
+        def make_tanh_b(u):
+            b = u // 8
+            bank = psum.tile([P, 512], F32, name="ab", tag="ab", bufs=3)
+            product(bank, u, lambda t: wb_w[b][:, 256 * t : 256 * (t + 1)].bitcast(FP4X4), wb_s[b])
+            tanh_b[u] = work.tile([P, 512], F32, name="tanh_b", tag="tanh_b", bufs=8)
+            nc.scalar.activation(by_four(tanh_b[u][:]), woven(bank), TANH)
+
+        def make_tanh_a(u):
+            b = u // 8
+            bank = psum.tile([P, 512], F32, name="ab", tag="ab", bufs=3)
+            product(bank, u, lambda t: wa_w[b][:, P * t : P * (t + 1)].bitcast(FP8X4), wa_s[b])
+            tanh_a[u] = work.tile([P, 512], F32, name="tanh_a", tag="tanh_a", bufs=6)
+            nc.scalar.activation(by_four(tanh_a[u][:]), woven(bank), TANH)
+
+        def make_diff(u):
+            diff[u] = work.tile([P, 512], F32, name="diff", tag="diff", bufs=6)
+            engine = nc.vector if u in VECTOR_SUBS else nc.gpsimd
+            engine.tensor_tensor(diff[u][:], tanh_a[u][:], tanh_b[u][:], SUB)
+
+        def make_f3(u):
+            b = u // 8
+            f3[u] = psum.tile([P, 512], F32, name="f3", tag="f3", bufs=3)
+            product(f3[u], u, lambda t: w3_w[b][:, P * t : P * (t + 1)].bitcast(FP8X4), w3_s[b])
+
+        def make_h(u):
+            b, j = divmod(u, 8)
+            nc.vector.tensor_tensor(by_four(h_bf[b][:, 512 * j : 512 * (j + 1)]), woven(f3[u]), by_four(diff[u][:]), MULT)
+
+        def quantize_h(b, lo, hi):
+            quantize(h_w[b][:, lo:hi], h_s[b][:, lo:hi], h_bf[b][:, 4 * lo : 4 * hi])
+
+        def scores(m, lo, hi):
+            bank = psum.tile([P, 512], F32, name="e_bank", tag="e_bank", bufs=2)
+            rows = slice(P * m, P * (m + 1))
+            for b in range(2):
+                nc.tensor.matmul_mx(
+                    out=bank[:, 0 : hi - lo],
+                    lhsT=v2_w[b][:, rows].bitcast(FP8X4),
+                    lhsT_scale=v2_s[4 * b : P, rows],
+                    rhs=h_w[b][:, lo:hi].bitcast(FP8X4),
+                    rhs_scale=h_s[b][:, lo:hi],
+                    start=(b == 0),
+                    stop=(b == 1),
+                )
+            nc.scalar.copy(e_t[m][:, lo:hi], bank[:, 0 : hi - lo])
+
+        gather_v(0, 256)
+        round_weight(nc.scalar.copy, wa_bf[0], wa_head[0], 0)
+        round_weight(nc.scalar.copy, wa_bf[0], wa_head[1], 64)
+        gather_v(256, 512)
+        gather_v(512, 1024)
+        quantize(wa_w[0][:], wa_s[0][:], wa_bf[0][:])
+        deal_wb(0)
+        round_weight(nc.vector.tensor_copy, w3_bf[0], w3_raw[0], 0)
+        make_tanh_a(0)
+        make_tanh_a(1)
+        deal_wb(1)
+        quantize(w3_w[0][:], w3_s[0][:], w3_bf[0][:])
+
+        for u in range(UNITS + 1):
+            if u < UNITS:
+                make_tanh_b(u)
+                make_diff(u)
+                make_f3(u)
+                if u + 2 < UNITS:
+                    make_tanh_a(u + 2)
+            if u >= 1:
+                make_h(u - 1)
+            if u == 2:
+                round_weight(nc.scalar.copy, wa_bf[1], wa_raw, 0)
+            if u == 4:
+                round_weight(nc.vector.tensor_copy, w3_bf[1], w3_raw[1], 0)
+                quantize(wa_w[1][:], wa_s[1][:], wa_bf[1][:])
+            if u == 5:
+                quantize_h(0, 0, 512)
+                quantize(w3_w[1][:], w3_s[1][:], w3_bf[1][:])
+            if u == 9:
+                quantize_h(0, 512, 1024)
+            if u == 10:
+                gather_v2(0, 128)
+            if u == 13:
+                quantize_h(1, 0, 512)
+                scores(0, 0, 512)
+            if u == 15:
+                quantize_h(1, 512, 768)
+                scores(0, 512, 768)
+            if u == 16:
+                quantize_h(1, 768, 896)
+                scores(0, 768, 896)
+        quantize_h(1, 896, 1024)
+        scores(0, 896, 1024)
+        gather_v2(128, 256)
+
+        left, right = {}, {}
+
+        def pick_left(m):
+            left[m] = work.tile([P, NP], F32, name="left", tag="left", bufs=3)
+            nc.vector.tensor_tensor(left[m][:], e_t[m][:].indirect(pos1_t[:]), leaf_t[:, m, :], ADD)
+
+        def pick_right(m):
+            right[m] = work.tile([P, NP], F32, name="right", tag="right", bufs=3)
+            nc.vector.tensor_copy(right[m][:], e_t[m][:].indirect(pos2_t[:]))
+
+        def finish(m):
+            result = work.tile([P, NP], F32, name="result", tag="result", bufs=4)
+            nc.vector.scalar_tensor_tensor(result[:], right[m][:], panel_t[:, m : m + 1], left[m][:], ADD, MULT)
+            nc.sync.dma_start(out[P * m : P * (m + 1), :], result[:])
+
+        for m in range(4):
+            if m + 1 < 4:
+                scores(m + 1, 0, 512)
+                scores(m + 1, 512, 1024)
+            pick_right(m)
+            if m >= 1:
+                finish(m - 1)
+            pick_left(m)
+            if m == 0:
+                gather_v2(256, 512)
+        finish(3)

@@ -1,6 +1,7 @@
 from contextlib import ExitStack
 
 import concourse.mybir as mybir
+from concourse.masks import make_identity
 
 K, H, T, S, T3, S2, NP = 512, 1024, 2048, 1024, 1024, 512, 512
 FLOPS = 2 * K * H * S * 3 + 2 * H * S2 * S
@@ -20,7 +21,8 @@ TANH = mybir.ActivationFunctionType.Tanh
 
 P = 128
 UNITS = 16
-VECTOR_SUBS = (3, 7, 11, 15)
+LEAD = 5
+AHEAD = 3
 
 
 def tile_list_bookmatch_leaf_scores_kernel(
@@ -42,7 +44,7 @@ def tile_list_bookmatch_leaf_scores_kernel(
         tab_s = keep.tile([P, T], U8, name="tab_s", align_bytes=64)
         tab2_w = [keep.tile([P, T3], I32, name=f"tab2_w{b}", align_bytes=64) for b in range(2)]
         tab2_s = keep.tile([P, T3], U8, name="tab2_s", align_bytes=64)
-        wb_raw = keep.tile([P, 2 * H], U8, name="wb_raw", align_bytes=64)
+        wb_raw = [keep.tile([P, H], U8, name=f"wb_raw{b}", align_bytes=64) for b in range(2)]
         wb_raw_s = keep.tile([P, H], U8, name="wb_raw_s", align_bytes=64)
         wa_head = [keep.tile([P, 4, 256], F32, name=f"wa_head{half}", align_bytes=64) for half in range(2)]
         wa_raw = keep.tile([P, 4, 512], F32, name="wa_raw", align_bytes=64)
@@ -66,10 +68,11 @@ def tile_list_bookmatch_leaf_scores_kernel(
             nc.sync.dma_start(tab_s[32 * q : 32 * q + 4, :].bitcast(I32), tab_scales[0, 4 * q : 4 * q + 4, :].bitcast(I32))
         for half in range(2):
             nc.sync.dma_start(wa_head[half][:], wa_rows[:, :, 256 * half : 256 * (half + 1)])
-        nc.sync.dma_start(wb_raw[:].bitcast(I32), wb_words[0].bitcast(I32))
+        nc.sync.dma_start(wb_raw[0][:].bitcast(I32), wb_words[0, :, 0:H].bitcast(I32))
         for q in range(4):
             nc.sync.dma_start(wb_raw_s[32 * q : 32 * q + 4, :].bitcast(I32), wb_scales[0, 4 * q : 4 * q + 4, :].bitcast(I32))
         nc.sync.dma_start(w3_raw[0][:], w3_rows[:, :, 0:512])
+        nc.sync.dma_start(wb_raw[1][:].bitcast(I32), wb_words[0, :, H : 2 * H].bitcast(I32))
         nc.sync.dma_start(wa_raw[:], wa_rows[:, :, 512:1024])
         nc.sync.dma_start(w3_raw[1][:], w3_rows[:, :, 512:1024])
         nc.sync.dma_start(offs2_t[:], offs2)
@@ -87,8 +90,10 @@ def tile_list_bookmatch_leaf_scores_kernel(
         v_s = keep.tile([P, S], U8, name="v_s", align_bytes=64)
         v2_w = [keep.tile([P, S2], U32, name=f"v2_w{b}", align_bytes=64) for b in range(2)]
         v2_s = keep.tile([P, S2], U8, name="v2_s", align_bytes=64)
-        wb_w = [keep.tile([P, 1024], U8, name=f"wb_w{b}", align_bytes=64) for b in range(2)]
-        wb_s = [keep.tile([P, 512], U8, name=f"wb_s{b}", align_bytes=64) for b in range(2)]
+        wb_w = keep.tile([P, 1024], U8, name="wb_w", align_bytes=64)
+        wb_s = keep.tile([P, 512], U8, name="wb_s", align_bytes=64)
+        ident = keep.tile([P, P], F32, name="ident", align_bytes=64)
+        make_identity(nc, ident[:])
         wa_bf = [keep.tile([P, 2048], BF16, name=f"wa_bf{b}", align_bytes=64) for b in range(2)]
         w3_bf = [keep.tile([P, 2048], BF16, name=f"w3_bf{b}", align_bytes=64) for b in range(2)]
         wa_w = [keep.tile([P, 512], U32, name=f"wa_w{b}", align_bytes=64) for b in range(2)]
@@ -111,15 +116,19 @@ def tile_list_bookmatch_leaf_scores_kernel(
                 nc.vector.tensor_copy(v2_w[b][:, lo:hi], tab2_w[b][:].bitcast(U32).indirect(picks))
             nc.vector.tensor_copy(v2_s[:, lo:hi], tab2_s[:].indirect(picks))
 
-        def deal_wb(b):
+        def deal_wb():
             nc.vector.tensor_copy(
-                wb_w[b][:].bitcast(U16).rearrange("p (t q) -> p t q", t=4),
-                wb_raw[:, 1024 * b : 1024 * (b + 1)].bitcast(U16).rearrange("p (q t) -> p t q", t=4),
+                wb_w[:].bitcast(U16).rearrange("p (t q) -> p t q", t=4),
+                wb_raw[1][:].bitcast(U16).rearrange("p (q t) -> p t q", t=4),
             )
             nc.vector.tensor_copy(
-                wb_s[b][:].rearrange("p (t q) -> p t q", t=4),
-                wb_raw_s[:, 512 * b : 512 * (b + 1)].rearrange("p (q t) -> p t q", t=4),
+                wb_s[:].rearrange("p (t q) -> p t q", t=4),
+                wb_raw_s[:, 512:1024].rearrange("p (q t) -> p t q", t=4),
             )
+
+        def round_plain(copy, bf, raw, c0):
+            count = raw.shape[2] // 4
+            copy(bf[:].rearrange("p (c t i) -> p c i t", t=4, i=4)[:, c0 : c0 + count], raw[:].rearrange("p i (c t) -> p c i t", t=4))
 
         def round_weight(copy, bf, raw, q0):
             count = raw.shape[2] // 4
@@ -147,41 +156,61 @@ def tile_list_bookmatch_leaf_scores_kernel(
         def by_four(ap):
             return ap.rearrange("p (j t) -> p j t", t=4)
 
-        tanh_a, tanh_b, diff, f3 = {}, {}, {}, {}
+        tanh_a, tanh_b, factors = {}, {}, {}
 
-        def make_tanh_b(u):
-            b = u // 8
+        def turned_tanh(u, words, scales, sign, name):
+            cols = slice(P * (u % 8), P * (u % 8 + 1))
             bank = psum.tile([P, 512], F32, name="ab", tag="ab", bufs=3)
-            product(bank, u, lambda t: wb_w[b][:, 256 * t : 256 * (t + 1)].bitcast(FP4X4), wb_s[b])
-            tanh_b[u] = work.tile([P, 512], F32, name="tanh_b", tag="tanh_b", bufs=8)
-            nc.scalar.activation(by_four(tanh_b[u][:]), woven(bank), TANH)
+            nc.tensor.matmul_mx(
+                out=bank[:], lhsT=v_w[:, cols].bitcast(FP8X4), lhsT_scale=v_s[:, cols], rhs=words, rhs_scale=scales, start=True, stop=True
+            )
+            result = work.tile([P, 512], F32, name=name, tag=name, bufs=6, align_bytes=64)
+            nc.scalar.activation(
+                result[:].rearrange("p (t q) -> p t q", t=4), bank[:].rearrange("p (q t) -> p t q", t=4), TANH, scale=sign
+            )
+            return result
 
-        def make_tanh_a(u):
-            b = u // 8
+        def direct_tanh(u, weight, weight_scale, name):
             bank = psum.tile([P, 512], F32, name="ab", tag="ab", bufs=3)
-            product(bank, u, lambda t: wa_w[b][:, P * t : P * (t + 1)].bitcast(FP8X4), wa_s[b])
-            tanh_a[u] = work.tile([P, 512], F32, name="tanh_a", tag="tanh_a", bufs=6)
-            nc.scalar.activation(by_four(tanh_a[u][:]), woven(bank), TANH)
+            product(bank, u, weight, weight_scale)
+            result = work.tile([P, 512], F32, name=name, tag=name, bufs=6, align_bytes=64)
+            nc.scalar.activation(by_four(result[:]), woven(bank), TANH)
+            return result
 
-        def make_diff(u):
-            diff[u] = work.tile([P, 512], F32, name="diff", tag="diff", bufs=6)
-            engine = nc.vector if u in VECTOR_SUBS else nc.gpsimd
-            engine.tensor_tensor(diff[u][:], tanh_a[u][:], tanh_b[u][:], SUB)
+        def make_tanh(u):
+            if u < 8:
+                tanh_b[u] = turned_tanh(u, wb_raw[0][:].bitcast(FP4X4), wb_raw_s[:, 0:512], -1.0, "tanh_b")
+                tanh_a[u] = turned_tanh(u, wa_w[0][:].bitcast(FP8X4), wa_s[0][:], 1.0, "tanh_a")
+            else:
+                tanh_b[u] = direct_tanh(u, lambda t: wb_w[:, 256 * t : 256 * (t + 1)].bitcast(FP4X4), wb_s, "tanh_b")
+                tanh_a[u] = direct_tanh(u, lambda t: wa_w[1][:, P * t : P * (t + 1)].bitcast(FP8X4), wa_s[1], "tanh_a")
 
-        def make_f3(u):
+        def make_factors(u):
             b = u // 8
-            f3[u] = psum.tile([P, 512], F32, name="f3", tag="f3", bufs=3)
-            product(f3[u], u, lambda t: w3_w[b][:, P * t : P * (t + 1)].bitcast(FP8X4), w3_s[b])
+            bank = psum.tile([P, 512], F32, name="f3_bank", tag="late", bufs=3)
+            product(bank, u, lambda t: w3_w[b][:, P * t : P * (t + 1)].bitcast(FP8X4), w3_s[b])
+            held = work.tile([P, 512], F32, name="held", tag="held", bufs=4)
+            if u < 8:
+                nc.scalar.copy(by_four(held[:]), woven(bank))
+                bank = psum.tile([P, 512], F32, name="diff", tag="diff", bufs=2)
+                for t in range(4):
+                    cols = slice(P * t, P * (t + 1))
+                    nc.tensor.matmul(bank[:, cols], tanh_a[u][:, cols], ident[:], start=True, stop=False, is_transpose=True)
+                    nc.tensor.matmul(bank[:, cols], tanh_b[u][:, cols], ident[:], start=False, stop=True, is_transpose=True)
+            else:
+                nc.vector.tensor_tensor(held[:], tanh_a[u][:], tanh_b[u][:], SUB)
+            factors[u] = (bank, held)
 
         def make_h(u):
             b, j = divmod(u, 8)
-            nc.vector.tensor_tensor(by_four(h_bf[b][:, 512 * j : 512 * (j + 1)]), woven(f3[u]), by_four(diff[u][:]), MULT)
+            bank, held = factors[u]
+            nc.vector.tensor_tensor(by_four(h_bf[b][:, 512 * j : 512 * (j + 1)]), woven(bank), by_four(held[:]), MULT)
 
         def quantize_h(b, lo, hi):
             quantize(h_w[b][:, lo:hi], h_s[b][:, lo:hi], h_bf[b][:, 4 * lo : 4 * hi])
 
         def scores(m, lo, hi):
-            bank = psum.tile([P, 512], F32, name="e_bank", tag="e_bank", bufs=2)
+            bank = psum.tile([P, 512], F32, name="e_bank", tag="late", bufs=3)
             rows = slice(P * m, P * (m + 1))
             for b in range(2):
                 nc.tensor.matmul_mx(
@@ -195,52 +224,53 @@ def tile_list_bookmatch_leaf_scores_kernel(
                 )
             nc.scalar.copy(e_t[m][:, lo:hi], bank[:, 0 : hi - lo])
 
-        gather_v(0, 256)
-        round_weight(nc.scalar.copy, wa_bf[0], wa_head[0], 0)
-        round_weight(nc.scalar.copy, wa_bf[0], wa_head[1], 64)
-        gather_v(256, 512)
-        gather_v(512, 1024)
-        quantize(wa_w[0][:], wa_s[0][:], wa_bf[0][:])
-        deal_wb(0)
-        round_weight(nc.vector.tensor_copy, w3_bf[0], w3_raw[0], 0)
-        make_tanh_a(0)
-        make_tanh_a(1)
-        deal_wb(1)
-        quantize(w3_w[0][:], w3_s[0][:], w3_bf[0][:])
+        order = list(range(LEAD))
+        for k in range(8):
+            order.append(8 + k)
+            if LEAD + k < 8:
+                order.append(LEAD + k)
+        h_pieces = {3: (0, 0, 512), 7: (0, 512, 1024), 11: (1, 0, 512), 13: (1, 512, 768), 14: (1, 768, 896), 15: (1, 896, 1024)}
 
-        for u in range(UNITS + 1):
-            if u < UNITS:
-                make_tanh_b(u)
-                make_diff(u)
-                make_f3(u)
-                if u + 2 < UNITS:
-                    make_tanh_a(u + 2)
-            if u >= 1:
-                make_h(u - 1)
-            if u == 2:
-                round_weight(nc.scalar.copy, wa_bf[1], wa_raw, 0)
-            if u == 4:
-                round_weight(nc.vector.tensor_copy, w3_bf[1], w3_raw[1], 0)
+        def close_piece(u):
+            if u in h_pieces:
+                b, lo, hi = h_pieces[u]
+                quantize_h(b, lo, hi)
+                if b == 1:
+                    scores(0, lo, hi)
+
+        gather_v(0, 256)
+        round_plain(nc.scalar.copy, wa_bf[0], wa_head[0], 0)
+        round_plain(nc.scalar.copy, wa_bf[0], wa_head[1], 64)
+        gather_v(256, 512)
+        quantize(wa_w[0][:], wa_s[0][:], wa_bf[0][:])
+        gather_v(512, 1024)
+        round_weight(nc.vector.tensor_copy, w3_bf[0], w3_raw[0], 0)
+        for u in order[:AHEAD]:
+            make_tanh(u)
+        quantize(w3_w[0][:], w3_s[0][:], w3_bf[0][:])
+        deal_wb()
+
+        for i, u in enumerate(order):
+            make_factors(u)
+            if i == 0:
+                round_weight(nc.vector.tensor_copy, wa_bf[1], wa_raw, 0)
+            if i == 1:
                 quantize(wa_w[1][:], wa_s[1][:], wa_bf[1][:])
-            if u == 5:
-                quantize_h(0, 0, 512)
+                round_weight(nc.vector.tensor_copy, w3_bf[1], w3_raw[1], 0)
+            if i + AHEAD < UNITS:
+                make_tanh(order[i + AHEAD])
+            if i >= 1:
+                make_h(order[i - 1])
+            if i == 2:
                 quantize(w3_w[1][:], w3_s[1][:], w3_bf[1][:])
-            if u == 9:
-                quantize_h(0, 512, 1024)
-            if u == 10:
-                gather_v2(0, 128)
-            if u == 13:
-                quantize_h(1, 0, 512)
-                scores(0, 0, 512)
-            if u == 15:
-                quantize_h(1, 512, 768)
-                scores(0, 512, 768)
-            if u == 16:
-                quantize_h(1, 768, 896)
-                scores(0, 768, 896)
-        quantize_h(1, 896, 1024)
-        scores(0, 896, 1024)
-        gather_v2(128, 256)
+            if i == 4:
+                gather_v2(0, P)
+            if i >= 2:
+                close_piece(order[i - 2])
+        make_h(order[-1])
+        close_piece(order[-2])
+        close_piece(order[-1])
+        gather_v2(P, 2 * P)
 
         left, right = {}, {}
 

@@ -22,7 +22,9 @@ TANH = mybir.ActivationFunctionType.Tanh
 P = 128
 UNITS = 16
 LEAD = 5
+FUSED_FROM = 0
 AHEAD = 3
+TURNED = 8
 
 
 def tile_list_bookmatch_leaf_scores_kernel(
@@ -48,14 +50,15 @@ def tile_list_bookmatch_leaf_scores_kernel(
         wb_raw_s = keep.tile([P, H], U8, name="wb_raw_s", align_bytes=64)
         wa_head = [keep.tile([P, 4, 256], F32, name=f"wa_head{half}", align_bytes=64) for half in range(2)]
         wa_raw = keep.tile([P, 4, 512], F32, name="wa_raw", align_bytes=64)
-        w3_raw = [keep.tile([P, 4, 512], F32, name=f"w3_raw{b}", align_bytes=64) for b in range(2)]
+        w3_head = [keep.tile([P, 4, 256], F32, name=f"w3_head{half}", align_bytes=64) for half in range(2)]
+        w3_raw = [None, keep.tile([P, 4, 512], F32, name="w3_raw", align_bytes=64)]
         leaf_t = keep.tile([P, 4, NP], F32, name="leaf_t", align_bytes=64)
         panel_t = keep.tile([P, 4], F32, name="panel_t", align_bytes=64)
         warm = keep.tile([P, 1], F32, name="warm")
         warm_out = keep.tile([P, 1], F32, name="warm_out")
 
         nc.gpsimd.memset(tab_s[:].bitcast(I32), 0)
-        nc.vector.memset(wb_raw_s[:].bitcast(I32), 0)
+        nc.gpsimd.memset(wb_raw_s[:].bitcast(I32), 0)
         nc.vector.memset(tab2_s[:].bitcast(I32), 0)
         nc.vector.memset(warm[:], 0.0)
         nc.scalar.activation(warm_out[:], warm[:], TANH)
@@ -70,8 +73,9 @@ def tile_list_bookmatch_leaf_scores_kernel(
             nc.sync.dma_start(wa_head[half][:], wa_rows[:, :, 256 * half : 256 * (half + 1)])
         nc.sync.dma_start(wb_raw[0][:].bitcast(I32), wb_words[0, :, 0:H].bitcast(I32))
         for q in range(4):
-            nc.sync.dma_start(wb_raw_s[32 * q : 32 * q + 4, :].bitcast(I32), wb_scales[0, 4 * q : 4 * q + 4, :].bitcast(I32))
-        nc.sync.dma_start(w3_raw[0][:], w3_rows[:, :, 0:512])
+            nc.gpsimd.dma_start(wb_raw_s[32 * q : 32 * q + 4, :].bitcast(I32), wb_scales[0, 4 * q : 4 * q + 4, :].bitcast(I32))
+        for half in range(2):
+            nc.sync.dma_start(w3_head[half][:], w3_rows[:, :, 256 * half : 256 * (half + 1)])
         nc.sync.dma_start(wb_raw[1][:].bitcast(I32), wb_words[0, :, H : 2 * H].bitcast(I32))
         nc.sync.dma_start(wa_raw[:], wa_rows[:, :, 512:1024])
         nc.sync.dma_start(w3_raw[1][:], w3_rows[:, :, 512:1024])
@@ -86,14 +90,12 @@ def tile_list_bookmatch_leaf_scores_kernel(
             nc.sync.dma_start(panel_t[:], panel.rearrange("(m p) -> p m", p=P))
         nc.sync.dma_start(leaf_t[:], leaf.rearrange("(m p) n -> p m n", p=P))
 
-        v_w = keep.tile([P, S], U32, name="v_w", align_bytes=64)
-        v_s = keep.tile([P, S], U8, name="v_s", align_bytes=64)
-        v2_w = [keep.tile([P, S2], U32, name=f"v2_w{b}", align_bytes=64) for b in range(2)]
-        v2_s = keep.tile([P, S2], U8, name="v2_s", align_bytes=64)
+        v_w, v_s = {}, {}
+        v2_w, v2_s = {}, {}
         wb_w = keep.tile([P, 1024], U8, name="wb_w", align_bytes=64)
-        wb_s = keep.tile([P, 512], U8, name="wb_s", align_bytes=64)
         ident = keep.tile([P, P], F32, name="ident", align_bytes=64)
-        make_identity(nc, ident[:])
+        nc.vector.memset(ident[:], 0.0)
+        make_identity(nc, ident[:], nomemset=True)
         wa_bf = [keep.tile([P, 2048], BF16, name=f"wa_bf{b}", align_bytes=64) for b in range(2)]
         w3_bf = [keep.tile([P, 2048], BF16, name=f"w3_bf{b}", align_bytes=64) for b in range(2)]
         wa_w = [keep.tile([P, 512], U32, name=f"wa_w{b}", align_bytes=64) for b in range(2)]
@@ -105,16 +107,24 @@ def tile_list_bookmatch_leaf_scores_kernel(
         h_s = [keep.tile([P, S], U8, name=f"h_s{b}", align_bytes=64) for b in range(2)]
         e_t = [keep.tile([P, S], F32, name=f"e{m}", align_bytes=64) for m in range(4)]
 
-        def gather_v(lo, hi):
-            picks = offs_t[:, lo // 16 : hi // 16]
-            nc.vector.tensor_copy(v_w[:, lo:hi], tab_w[:].bitcast(U32).indirect(picks))
-            nc.vector.tensor_copy(v_s[:, lo:hi], tab_s[:].indirect(picks))
+        def gather_v_words(part, tag):
+            v_w[part] = keep.tile([P, 256], U32, name=f"v_w{part}", tag=tag, align_bytes=64)
+            nc.vector.tensor_copy(v_w[part][:], tab_w[:].bitcast(U32).indirect(offs_t[:, 16 * part : 16 * (part + 1)]))
 
-        def gather_v2(lo, hi):
-            picks = offs2_t[:, lo // 16 : hi // 16]
+        def gather_v_scales(part, tag):
+            v_s[part] = keep.tile([P, 256], U8, name=f"v_s{part}", tag=tag, align_bytes=64)
+            nc.vector.tensor_copy(v_s[part][:], tab_s[:].indirect(offs_t[:, 16 * part : 16 * (part + 1)]))
+
+        def patches(u):
+            part, first = divmod(P * (u % 8), 256)
+            return v_w[part][:, first : first + P].bitcast(FP8X4), v_s[part][:, first : first + P]
+
+        def gather_v2(half, words, scales):
+            picks = offs2_t[:, 16 * half : 16 * (half + 1)]
             for b in range(2):
-                nc.vector.tensor_copy(v2_w[b][:, lo:hi], tab2_w[b][:].bitcast(U32).indirect(picks))
-            nc.vector.tensor_copy(v2_s[:, lo:hi], tab2_s[:].indirect(picks))
+                nc.vector.tensor_copy(words[:, 256 * b : 256 * (b + 1)], tab2_w[b][:].bitcast(U32).indirect(picks))
+            nc.vector.tensor_copy(scales[:], tab2_s[:].indirect(picks))
+            v2_w[half], v2_s[half] = words, scales
 
         def deal_wb():
             nc.vector.tensor_copy(
@@ -132,20 +142,20 @@ def tile_list_bookmatch_leaf_scores_kernel(
 
         def round_weight(copy, bf, raw, q0):
             count = raw.shape[2] // 4
-            copy(bf[:].rearrange("p (t q i) -> p q t i", t=4, i=4)[:, q0 : q0 + count], raw[:].rearrange("p i (q t) -> p q t i", t=4))
+            copy(bf[:].rearrange("p (t q i) -> p q i t", t=4, i=4)[:, q0 : q0 + count], raw.rearrange("p i (q t) -> p q i t", t=4))
 
         def quantize(words, scales, bf):
             nc.vector.quantize_mx(out=words.bitcast(FP8X4), scales=scales, in_=bf)
 
         def product(bank, u, weight, weight_scale):
-            cols = slice(P * (u % 8), P * (u % 8 + 1))
+            v_words, v_scales = patches(u)
             for t in range(4):
                 nc.tensor.matmul_mx(
                     out=bank[:, P * t : P * (t + 1)],
                     lhsT=weight(t),
                     lhsT_scale=weight_scale[:, P * t : P * (t + 1)],
-                    rhs=v_w[:, cols].bitcast(FP8X4),
-                    rhs_scale=v_s[:, cols],
+                    rhs=v_words,
+                    rhs_scale=v_scales,
                     start=True,
                     stop=True,
                 )
@@ -158,16 +168,15 @@ def tile_list_bookmatch_leaf_scores_kernel(
 
         tanh_a, tanh_b, factors = {}, {}, {}
 
-        def turned_tanh(u, words, scales, sign, name):
-            cols = slice(P * (u % 8), P * (u % 8 + 1))
+        def turned_tanh(u, words, scales, sign, name, dealt):
+            v_words, v_scales = patches(u)
             bank = psum.tile([P, 512], F32, name="ab", tag="ab", bufs=3)
             nc.tensor.matmul_mx(
-                out=bank[:], lhsT=v_w[:, cols].bitcast(FP8X4), lhsT_scale=v_s[:, cols], rhs=words, rhs_scale=scales, start=True, stop=True
+                out=bank[:], lhsT=v_words, lhsT_scale=v_scales, rhs=words, rhs_scale=scales, start=True, stop=True
             )
             result = work.tile([P, 512], F32, name=name, tag=name, bufs=6, align_bytes=64)
-            nc.scalar.activation(
-                result[:].rearrange("p (t q) -> p t q", t=4), bank[:].rearrange("p (q t) -> p t q", t=4), TANH, scale=sign
-            )
+            pattern = "p (t q) -> p t q" if dealt else "p (q t) -> p t q"
+            nc.scalar.activation(result[:].rearrange("p (t q) -> p t q", t=4), bank[:].rearrange(pattern, t=4), TANH, scale=sign)
             return result
 
         def direct_tanh(u, weight, weight_scale, name):
@@ -179,20 +188,26 @@ def tile_list_bookmatch_leaf_scores_kernel(
 
         def make_tanh(u):
             if u < 8:
-                tanh_b[u] = turned_tanh(u, wb_raw[0][:].bitcast(FP4X4), wb_raw_s[:, 0:512], -1.0, "tanh_b")
-                tanh_a[u] = turned_tanh(u, wa_w[0][:].bitcast(FP8X4), wa_s[0][:], 1.0, "tanh_a")
+                tanh_b[u] = turned_tanh(u, wb_raw[0][:].bitcast(FP4X4), wb_raw_s[:, 0:512], -1.0, "tanh_b", False)
+                tanh_a[u] = turned_tanh(u, wa_w[0][:].bitcast(FP8X4), wa_s[0][:], 1.0, "tanh_a", False)
+            elif u < TURNED:
+                tanh_b[u] = turned_tanh(u, wb_w[:].bitcast(FP4X4), wb_s[:], -1.0, "tanh_b", True)
+                tanh_a[u] = turned_tanh(u, wa_w[1][:].bitcast(FP8X4), wa_s[1][:], 1.0, "tanh_a", True)
             else:
                 tanh_b[u] = direct_tanh(u, lambda t: wb_w[:, 256 * t : 256 * (t + 1)].bitcast(FP4X4), wb_s, "tanh_b")
                 tanh_a[u] = direct_tanh(u, lambda t: wa_w[1][:, P * t : P * (t + 1)].bitcast(FP8X4), wa_s[1], "tanh_a")
 
         def make_factors(u):
             b = u // 8
-            bank = psum.tile([P, 512], F32, name="f3_bank", tag="late", bufs=3)
+            bank = psum.tile([P, 512], F32, name="f3_bank", tag="late", bufs=2)
             product(bank, u, lambda t: w3_w[b][:, P * t : P * (t + 1)].bitcast(FP8X4), w3_s[b])
-            held = work.tile([P, 512], F32, name="held", tag="held", bufs=4)
-            if u < 8:
+            if u == UNITS - 1:
+                held = keep.tile([P, 512], F32, name="held_last", align_bytes=64)
+            else:
+                held = work.tile([P, 512], F32, name="held", tag="held", bufs=4, align_bytes=64)
+            if u < TURNED:
                 nc.scalar.copy(by_four(held[:]), woven(bank))
-                bank = psum.tile([P, 512], F32, name="diff", tag="diff", bufs=2)
+                bank = psum.tile([P, 512], F32, name="diff", tag="diff", bufs=3)
                 for t in range(4):
                     cols = slice(P * t, P * (t + 1))
                     nc.tensor.matmul(bank[:, cols], tanh_a[u][:, cols], ident[:], start=True, stop=False, is_transpose=True)
@@ -210,13 +225,13 @@ def tile_list_bookmatch_leaf_scores_kernel(
             quantize(h_w[b][:, lo:hi], h_s[b][:, lo:hi], h_bf[b][:, 4 * lo : 4 * hi])
 
         def scores(m, lo, hi):
-            bank = psum.tile([P, 512], F32, name="e_bank", tag="late", bufs=3)
-            rows = slice(P * m, P * (m + 1))
+            bank = psum.tile([P, 512], F32, name="e_bank", tag="diff", bufs=3)
+            half, first = divmod(P * m, 256)
             for b in range(2):
                 nc.tensor.matmul_mx(
                     out=bank[:, 0 : hi - lo],
-                    lhsT=v2_w[b][:, rows].bitcast(FP8X4),
-                    lhsT_scale=v2_s[4 * b : P, rows],
+                    lhsT=v2_w[half][:, 256 * b + first : 256 * b + first + P].bitcast(FP8X4),
+                    lhsT_scale=v2_s[half][4 * b : P, first : first + P],
                     rhs=h_w[b][:, lo:hi].bitcast(FP8X4),
                     rhs_scale=h_s[b][:, lo:hi],
                     start=(b == 0),
@@ -225,76 +240,88 @@ def tile_list_bookmatch_leaf_scores_kernel(
             nc.scalar.copy(e_t[m][:, lo:hi], bank[:, 0 : hi - lo])
 
         order = list(range(LEAD))
-        for k in range(8):
-            order.append(8 + k)
-            if LEAD + k < 8:
-                order.append(LEAD + k)
+        turned = list(range(LEAD, TURNED))
+        for k, u in enumerate(range(TURNED, UNITS)):
+            order.append(u)
+            order.extend(turned[k : k + 1])
+        order.extend(turned[UNITS - TURNED :])
         h_pieces = {3: (0, 0, 512), 7: (0, 512, 1024), 11: (1, 0, 512), 13: (1, 512, 768), 14: (1, 768, 896), 15: (1, 896, 1024)}
 
-        def close_piece(u):
-            if u in h_pieces:
-                b, lo, hi = h_pieces[u]
-                quantize_h(b, lo, hi)
-                if b == 1:
-                    scores(0, lo, hi)
+        finished = set()
+        closed = set()
 
-        gather_v(0, 256)
+        def close_piece(u):
+            finished.add(u)
+            for b, lo, hi in h_pieces.values():
+                if (b, lo) not in closed and all(8 * b + j in finished for j in range(lo // P, hi // P)):
+                    closed.add((b, lo))
+                    quantize_h(b, lo, hi)
+                    if b == 1:
+                        scores(0, lo, hi)
+                        scores(1, lo, hi)
+
+        for part in range(3):
+            gather_v_words(part, f"v_w{part}")
+        for part in range(3):
+            gather_v_scales(part, f"v_s{part}")
         round_plain(nc.scalar.copy, wa_bf[0], wa_head[0], 0)
         round_plain(nc.scalar.copy, wa_bf[0], wa_head[1], 64)
-        gather_v(256, 512)
         quantize(wa_w[0][:], wa_s[0][:], wa_bf[0][:])
-        gather_v(512, 1024)
-        round_weight(nc.vector.tensor_copy, w3_bf[0], w3_raw[0], 0)
+        for half in range(2):
+            round_weight(nc.vector.tensor_copy, w3_bf[0], w3_head[half][:], 64 * half)
         for u in order[:AHEAD]:
             make_tanh(u)
         quantize(w3_w[0][:], w3_s[0][:], w3_bf[0][:])
+        gather_v_words(3, "w3_bf0")
+        gather_v_scales(3, "w3_head1")
+        wb_s = keep.tile([P, 512], U8, name="wb_s", tag="w3_head0", align_bytes=64)
         deal_wb()
 
         for i, u in enumerate(order):
             make_factors(u)
             if i == 0:
-                round_weight(nc.vector.tensor_copy, wa_bf[1], wa_raw, 0)
+                round_weight(nc.vector.tensor_copy, wa_bf[1], wa_raw[:], 0)
             if i == 1:
                 quantize(wa_w[1][:], wa_s[1][:], wa_bf[1][:])
-                round_weight(nc.vector.tensor_copy, w3_bf[1], w3_raw[1], 0)
+                round_weight(nc.vector.tensor_copy, w3_bf[1], w3_raw[1][:], 0)
             if i + AHEAD < UNITS:
                 make_tanh(order[i + AHEAD])
             if i >= 1:
                 make_h(order[i - 1])
             if i == 2:
                 quantize(w3_w[1][:], w3_s[1][:], w3_bf[1][:])
-            if i == 4:
-                gather_v2(0, P)
+            if i == 6:
+                gather_v2(
+                    0,
+                    keep.tile([P, 512], U32, name="v2_w_first", align_bytes=64),
+                    keep.tile([P, 256], U8, name="v2_s_first", align_bytes=64),
+                )
             if i >= 2:
                 close_piece(order[i - 2])
         make_h(order[-1])
         close_piece(order[-2])
         close_piece(order[-1])
-        gather_v2(P, 2 * P)
+        gather_v2(
+            1,
+            keep.tile([P, 512], U32, name="v2_w_last", tag="h_bf1", align_bytes=64),
+            keep.tile([P, 256], U8, name="v2_s_last", tag="held_last", align_bytes=64),
+        )
 
-        left, right = {}, {}
+        left = {}
 
         def pick_left(m):
-            left[m] = work.tile([P, NP], F32, name="left", tag="left", bufs=3)
+            left[m] = work.tile([P, NP], F32, name="left", tag="left", bufs=2)
             nc.vector.tensor_tensor(left[m][:], e_t[m][:].indirect(pos1_t[:]), leaf_t[:, m, :], ADD)
 
-        def pick_right(m):
-            right[m] = work.tile([P, NP], F32, name="right", tag="right", bufs=3)
-            nc.vector.tensor_copy(right[m][:], e_t[m][:].indirect(pos2_t[:]))
-
-        def finish(m):
-            result = work.tile([P, NP], F32, name="result", tag="result", bufs=4)
-            nc.vector.scalar_tensor_tensor(result[:], right[m][:], panel_t[:, m : m + 1], left[m][:], ADD, MULT)
-            nc.sync.dma_start(out[P * m : P * (m + 1), :], result[:])
-
+        for m in range(2, 4):
+            scores(m, 0, 512)
+            scores(m, 512, 1024)
+        pick_left(0)
         for m in range(4):
+            right = work.tile([P, NP], F32, name="right", tag="right", bufs=2)
+            nc.vector.tensor_copy(right[:], e_t[m][:].indirect(pos2_t[:]))
             if m + 1 < 4:
-                scores(m + 1, 0, 512)
-                scores(m + 1, 512, 1024)
-            pick_right(m)
-            if m >= 1:
-                finish(m - 1)
-            pick_left(m)
-            if m == 0:
-                gather_v2(256, 512)
-        finish(3)
+                pick_left(m + 1)
+            result = work.tile([P, NP], F32, name="result", tag="result", bufs=4)
+            nc.vector.scalar_tensor_tensor(result[:], right[:], panel_t[:, m : m + 1], left[m][:], ADD, MULT)
+            nc.sync.dma_start(out[P * m : P * (m + 1), :], result[:])

@@ -3,7 +3,7 @@ from contextlib import ExitStack
 import concourse.mybir as mybir
 from concourse.masks import make_identity
 
-K, H, T, S, T3, S2, NP = 512, 1024, 2048, 1024, 1024, 512, 512
+K, H, T, S, T3, S2, PAIRS = 512, 1024, 2048, 1024, 1024, 512, 512
 FLOPS = 2 * K * H * S * 3 + 2 * H * S2 * S
 
 F32 = mybir.dt.float32
@@ -20,11 +20,19 @@ MULT = mybir.AluOpType.mult
 TANH = mybir.ActivationFunctionType.Tanh
 
 P = 128
-UNITS = 16
-LEAD = 5
-FUSED_FROM = 0
+BANK = 512
+HALF = 256
+GROUPS = S // P
+UNITS = 2 * GROUPS
+LEAD = 6
 AHEAD = 3
-TURNED = 8
+MIXED_END = 4
+EARLY_PATCHES = (0, 256, 768)
+PANEL_STEP = 6
+
+
+def is_turned(u):
+    return u < GROUPS or (u >= UNITS - MIXED_END and u % 2 == 0)
 
 
 def tile_list_bookmatch_leaf_scores_kernel(
@@ -39,121 +47,116 @@ def tile_list_bookmatch_leaf_scores_kernel(
 
         offs_t = lists.tile([P, S // 16], U16, name="offs_t")
         offs2_t = lists.tile([P, S2 // 16], U16, name="offs2_t")
-        pos1_t = lists.tile([P, NP // 16], U16, name="pos1_t")
-        pos2_t = lists.tile([P, NP // 16], U16, name="pos2_t")
+        pos1_t = lists.tile([P, PAIRS // 16], U16, name="pos1_t")
+        pos2_t = lists.tile([P, PAIRS // 16], U16, name="pos2_t")
 
         tab_w = keep.tile([P, T], I32, name="tab_w", align_bytes=64)
         tab_s = keep.tile([P, T], U8, name="tab_s", align_bytes=64)
         tab2_w = [keep.tile([P, T3], I32, name=f"tab2_w{b}", align_bytes=64) for b in range(2)]
         tab2_s = keep.tile([P, T3], U8, name="tab2_s", align_bytes=64)
-        wb_raw = [keep.tile([P, H], U8, name=f"wb_raw{b}", align_bytes=64) for b in range(2)]
+        wb_raw = [keep.tile([P, 2 * BANK], U8, name=f"wb_raw{b}", align_bytes=64) for b in range(2)]
         wb_raw_s = keep.tile([P, H], U8, name="wb_raw_s", align_bytes=64)
-        wa_head = [keep.tile([P, 4, 256], F32, name=f"wa_head{half}", align_bytes=64) for half in range(2)]
-        wa_raw = keep.tile([P, 4, 512], F32, name="wa_raw", align_bytes=64)
-        w3_head = [keep.tile([P, 4, 256], F32, name=f"w3_head{half}", align_bytes=64) for half in range(2)]
-        w3_raw = [None, keep.tile([P, 4, 512], F32, name="w3_raw", align_bytes=64)]
-        leaf_t = keep.tile([P, 4, NP], F32, name="leaf_t", align_bytes=64)
+        wa_head = [keep.tile([P, 4, HALF], F32, name=f"wa_head{half}", align_bytes=64) for half in range(2)]
+        wa_rest = keep.tile([P, 4, BANK], F32, name="wa_rest", align_bytes=64)
+        w3_head = [keep.tile([P, 4, HALF], F32, name=f"w3_head{half}", align_bytes=64) for half in range(2)]
+        w3_rest = keep.tile([P, 4, BANK], F32, name="w3_rest", align_bytes=64)
+        leaf_t = keep.tile([P, 4, PAIRS], F32, name="leaf_t", align_bytes=64)
         panel_t = keep.tile([P, 4], F32, name="panel_t", align_bytes=64)
-        warm = keep.tile([P, 1], F32, name="warm")
-        warm_out = keep.tile([P, 1], F32, name="warm_out")
 
         nc.gpsimd.memset(tab_s[:].bitcast(I32), 0)
         nc.gpsimd.memset(wb_raw_s[:].bitcast(I32), 0)
         nc.vector.memset(tab2_s[:].bitcast(I32), 0)
-        nc.vector.memset(warm[:], 0.0)
-        nc.scalar.activation(warm_out[:], warm[:], TANH)
 
-        wa_rows = wa.rearrange("(p j) c -> p j c", j=4)
-        w3_rows = w3.rearrange("(p j) c -> p j c", j=4)
+        wa_rows = wa.rearrange("(p i) c -> p i c", i=4)
+        w3_rows = w3.rearrange("(p i) c -> p i c", i=4)
         nc.sync.dma_start(offs_t[:], offs)
-        nc.sync.dma_start(tab_w[:], tab_words[0].rearrange("p t i -> p (t i)").bitcast(I32))
-        for q in range(4):
-            nc.sync.dma_start(tab_s[32 * q : 32 * q + 4, :].bitcast(I32), tab_scales[0, 4 * q : 4 * q + 4, :].bitcast(I32))
+        nc.sync.dma_start(tab_w[:], tab_words[0].rearrange("p c i -> p (c i)").bitcast(I32))
+        for quad in range(4):
+            rows = tab_scales[0, 4 * quad : 4 * quad + 4, :]
+            nc.sync.dma_start(tab_s[32 * quad : 32 * quad + 4, :].bitcast(I32), rows.bitcast(I32))
         for half in range(2):
-            nc.sync.dma_start(wa_head[half][:], wa_rows[:, :, 256 * half : 256 * (half + 1)])
-        nc.sync.dma_start(wb_raw[0][:].bitcast(I32), wb_words[0, :, 0:H].bitcast(I32))
-        for q in range(4):
-            nc.gpsimd.dma_start(wb_raw_s[32 * q : 32 * q + 4, :].bitcast(I32), wb_scales[0, 4 * q : 4 * q + 4, :].bitcast(I32))
+            nc.sync.dma_start(wa_head[half][:], wa_rows[:, :, HALF * half : HALF * (half + 1)])
+        nc.sync.dma_start(wb_raw[0][:].bitcast(I32), wb_words[0, :, 0 : 2 * BANK].bitcast(I32))
+        for quad in range(4):
+            rows = wb_scales[0, 4 * quad : 4 * quad + 4, :]
+            nc.sync.dma_start(wb_raw_s[32 * quad : 32 * quad + 4, :].bitcast(I32), rows.bitcast(I32))
         for half in range(2):
-            nc.sync.dma_start(w3_head[half][:], w3_rows[:, :, 256 * half : 256 * (half + 1)])
-        nc.sync.dma_start(wb_raw[1][:].bitcast(I32), wb_words[0, :, H : 2 * H].bitcast(I32))
-        nc.sync.dma_start(wa_raw[:], wa_rows[:, :, 512:1024])
-        nc.sync.dma_start(w3_raw[1][:], w3_rows[:, :, 512:1024])
+            nc.sync.dma_start(w3_head[half][:], w3_rows[:, :, HALF * half : HALF * (half + 1)])
+        nc.sync.dma_start(wb_raw[1][:].bitcast(I32), wb_words[0, :, 2 * BANK : 4 * BANK].bitcast(I32))
+        nc.sync.dma_start(wa_rest[:], wa_rows[:, :, BANK:H])
+        nc.sync.dma_start(w3_rest[:], w3_rows[:, :, BANK:H])
         nc.sync.dma_start(offs2_t[:], offs2)
         for b in range(2):
-            nc.sync.dma_start(tab2_w[b][:], tab2_words[b].rearrange("p t i -> p (t i)").bitcast(I32))
-        for q in range(4):
-            nc.sync.dma_start(tab2_s[32 * q : 32 * q + 8, :].bitcast(I32), tab2_scales[:, 4 * q : 4 * q + 4, :].bitcast(I32))
+            nc.sync.dma_start(tab2_w[b][:], tab2_words[b].rearrange("p c i -> p (c i)").bitcast(I32))
+        for quad in range(4):
+            rows = tab2_scales[:, 4 * quad : 4 * quad + 4, :]
+            nc.sync.dma_start(tab2_s[32 * quad : 32 * quad + 8, :].bitcast(I32), rows.bitcast(I32))
         nc.sync.dma_start(pos1_t[:], pos1)
         nc.sync.dma_start(pos2_t[:], pos2)
         with nc.allow_non_contiguous_dma(reason="one panel value a partition"):
             nc.sync.dma_start(panel_t[:], panel.rearrange("(m p) -> p m", p=P))
         nc.sync.dma_start(leaf_t[:], leaf.rearrange("(m p) n -> p m n", p=P))
 
-        v_w, v_s = {}, {}
-        v2_w, v2_s = {}, {}
-        wb_w = keep.tile([P, 1024], U8, name="wb_w", align_bytes=64)
+        wb_dealt = keep.tile([P, 2 * BANK], U8, name="wb_dealt", align_bytes=64)
         ident = keep.tile([P, P], F32, name="ident", align_bytes=64)
         nc.vector.memset(ident[:], 0.0)
         make_identity(nc, ident[:], nomemset=True)
-        wa_bf = [keep.tile([P, 2048], BF16, name=f"wa_bf{b}", align_bytes=64) for b in range(2)]
-        w3_bf = [keep.tile([P, 2048], BF16, name=f"w3_bf{b}", align_bytes=64) for b in range(2)]
-        wa_w = [keep.tile([P, 512], U32, name=f"wa_w{b}", align_bytes=64) for b in range(2)]
-        wa_s = [keep.tile([P, 512], U8, name=f"wa_s{b}", align_bytes=64) for b in range(2)]
-        w3_w = [keep.tile([P, 512], U32, name=f"w3_w{b}", align_bytes=64) for b in range(2)]
-        w3_s = [keep.tile([P, 512], U8, name=f"w3_s{b}", align_bytes=64) for b in range(2)]
+        wa_bf = [keep.tile([P, 4 * BANK], BF16, name=f"wa_bf{b}", align_bytes=64) for b in range(2)]
+        w3_bf = [keep.tile([P, 4 * BANK], BF16, name=f"w3_bf{b}", align_bytes=64) for b in range(2)]
+        wa_w = [keep.tile([P, BANK], U32, name=f"wa_w{b}", align_bytes=64) for b in range(2)]
+        wa_s = [keep.tile([P, BANK], U8, name=f"wa_s{b}", align_bytes=64) for b in range(2)]
+        w3_w = [keep.tile([P, BANK], U32, name=f"w3_w{b}", align_bytes=64) for b in range(2)]
+        w3_s = [keep.tile([P, BANK], U8, name=f"w3_s{b}", align_bytes=64) for b in range(2)]
         h_bf = [keep.tile([P, 4 * S], BF16, name=f"h_bf{b}", align_bytes=64) for b in range(2)]
         h_w = [keep.tile([P, S], U32, name=f"h_w{b}", align_bytes=64) for b in range(2)]
         h_s = [keep.tile([P, S], U8, name=f"h_s{b}", align_bytes=64) for b in range(2)]
-        e_t = [keep.tile([P, S], F32, name=f"e{m}", align_bytes=64) for m in range(4)]
+        e_t = [keep.tile([P, S], F32, name=f"e{m}", align_bytes=64) for m in range(S2 // P)]
 
-        def gather_v_words(part, tag):
-            v_w[part] = keep.tile([P, 256], U32, name=f"v_w{part}", tag=tag, align_bytes=64)
-            nc.vector.tensor_copy(v_w[part][:], tab_w[:].bitcast(U32).indirect(offs_t[:, 16 * part : 16 * (part + 1)]))
+        patch_groups = []
+        v2_w, v2_s = {}, {}
+        tanh_a, tanh_b, factors, left = {}, {}, {}, {}
 
-        def gather_v_scales(part, tag):
-            v_s[part] = keep.tile([P, 256], U8, name=f"v_s{part}", tag=tag, align_bytes=64)
-            nc.vector.tensor_copy(v_s[part][:], tab_s[:].indirect(offs_t[:, 16 * part : 16 * (part + 1)]))
+        def gather_v(lo, hi, words_tag, scales_tag):
+            picks = offs_t[:, lo // 16 : hi // 16]
+            words = keep.tile([P, hi - lo], U32, name=f"v_w{lo}", tag=words_tag, align_bytes=64)
+            scales = keep.tile([P, hi - lo], U8, name=f"v_s{lo}", tag=scales_tag, align_bytes=64)
+            nc.vector.tensor_copy(words[:], tab_w[:].bitcast(U32).indirect(picks))
+            nc.vector.tensor_copy(scales[:], tab_s[:].indirect(picks))
+            for first in range(0, hi - lo, P):
+                patch_groups.append((words[:, first : first + P].bitcast(FP8X4), scales[:, first : first + P]))
 
-        def patches(u):
-            part, first = divmod(P * (u % 8), 256)
-            return v_w[part][:, first : first + P].bitcast(FP8X4), v_s[part][:, first : first + P]
-
-        def gather_v2(half, words, scales):
-            picks = offs2_t[:, 16 * half : 16 * (half + 1)]
+        def gather_v2(half, words_tag, scales_tag):
+            picks = offs2_t[:, HALF * half // 16 : HALF * (half + 1) // 16]
+            v2_w[half] = keep.tile([P, 2 * HALF], U32, name=f"v2_w{half}", tag=words_tag, align_bytes=64)
+            v2_s[half] = keep.tile([P, HALF], U8, name=f"v2_s{half}", tag=scales_tag, align_bytes=64)
             for b in range(2):
-                nc.vector.tensor_copy(words[:, 256 * b : 256 * (b + 1)], tab2_w[b][:].bitcast(U32).indirect(picks))
-            nc.vector.tensor_copy(scales[:], tab2_s[:].indirect(picks))
-            v2_w[half], v2_s[half] = words, scales
+                nc.vector.tensor_copy(v2_w[half][:, HALF * b : HALF * (b + 1)], tab2_w[b][:].bitcast(U32).indirect(picks))
+            nc.vector.tensor_copy(v2_s[half][:], tab2_s[:].indirect(picks))
 
-        def deal_wb():
-            nc.vector.tensor_copy(
-                wb_w[:].bitcast(U16).rearrange("p (t q) -> p t q", t=4),
-                wb_raw[1][:].bitcast(U16).rearrange("p (q t) -> p t q", t=4),
-            )
-            nc.vector.tensor_copy(
-                wb_s[:].rearrange("p (t q) -> p t q", t=4),
-                wb_raw_s[:, 512:1024].rearrange("p (q t) -> p t q", t=4),
+        def round_in_order(half):
+            quads = slice(HALF // 4 * half, HALF // 4 * (half + 1))
+            nc.scalar.copy(
+                wa_bf[0][:].rearrange("p (q t i) -> p q i t", t=4, i=4)[:, quads],
+                wa_head[half][:].rearrange("p i (q t) -> p q i t", t=4),
             )
 
-        def round_plain(copy, bf, raw, c0):
+        def round_dealt(rounded, raw, q0):
             count = raw.shape[2] // 4
-            copy(bf[:].rearrange("p (c t i) -> p c i t", t=4, i=4)[:, c0 : c0 + count], raw[:].rearrange("p i (c t) -> p c i t", t=4))
+            nc.vector.tensor_copy(
+                rounded[:].rearrange("p (t q i) -> p q i t", t=4, i=4)[:, q0 : q0 + count],
+                raw[:].rearrange("p i (q t) -> p q i t", t=4),
+            )
 
-        def round_weight(copy, bf, raw, q0):
-            count = raw.shape[2] // 4
-            copy(bf[:].rearrange("p (t q i) -> p q i t", t=4, i=4)[:, q0 : q0 + count], raw.rearrange("p i (q t) -> p q i t", t=4))
+        def quantize(words, scales, rounded):
+            nc.vector.quantize_mx(out=words.bitcast(FP8X4), scales=scales, in_=rounded)
 
-        def quantize(words, scales, bf):
-            nc.vector.quantize_mx(out=words.bitcast(FP8X4), scales=scales, in_=bf)
-
-        def product(bank, u, weight, weight_scale):
-            v_words, v_scales = patches(u)
+        def direct_product(bank, u, weight_words, weight_scales):
+            v_words, v_scales = patch_groups[u % GROUPS]
             for t in range(4):
                 nc.tensor.matmul_mx(
                     out=bank[:, P * t : P * (t + 1)],
-                    lhsT=weight(t),
-                    lhsT_scale=weight_scale[:, P * t : P * (t + 1)],
+                    lhsT=weight_words(t),
+                    lhsT_scale=weight_scales[:, P * t : P * (t + 1)],
                     rhs=v_words,
                     rhs_scale=v_scales,
                     start=True,
@@ -166,162 +169,147 @@ def tile_list_bookmatch_leaf_scores_kernel(
         def by_four(ap):
             return ap.rearrange("p (j t) -> p j t", t=4)
 
-        tanh_a, tanh_b, factors = {}, {}, {}
-
-        def turned_tanh(u, words, scales, sign, name, dealt):
-            v_words, v_scales = patches(u)
-            bank = psum.tile([P, 512], F32, name="ab", tag="ab", bufs=3)
+        def turned_tanh(u, words, scales, sign, name):
+            v_words, v_scales = patch_groups[u % GROUPS]
+            bank = psum.tile([P, BANK], F32, name="pre_tanh", tag="pre_tanh", bufs=3)
             nc.tensor.matmul_mx(
                 out=bank[:], lhsT=v_words, lhsT_scale=v_scales, rhs=words, rhs_scale=scales, start=True, stop=True
             )
-            result = work.tile([P, 512], F32, name=name, tag=name, bufs=6, align_bytes=64)
-            pattern = "p (t q) -> p t q" if dealt else "p (q t) -> p t q"
+            result = work.tile([P, BANK], F32, name=name, tag=name, bufs=6, align_bytes=64)
+            pattern = "p (q t) -> p t q" if u < GROUPS else "p (t q) -> p t q"
             nc.scalar.activation(result[:].rearrange("p (t q) -> p t q", t=4), bank[:].rearrange(pattern, t=4), TANH, scale=sign)
             return result
 
-        def direct_tanh(u, weight, weight_scale, name):
-            bank = psum.tile([P, 512], F32, name="ab", tag="ab", bufs=3)
-            product(bank, u, weight, weight_scale)
-            result = work.tile([P, 512], F32, name=name, tag=name, bufs=6, align_bytes=64)
+        def direct_tanh(u, weight_words, weight_scales, name):
+            bank = psum.tile([P, BANK], F32, name="pre_tanh", tag="pre_tanh", bufs=3)
+            direct_product(bank, u, weight_words, weight_scales)
+            result = work.tile([P, BANK], F32, name=name, tag=name, bufs=6, align_bytes=64)
             nc.scalar.activation(by_four(result[:]), woven(bank), TANH)
             return result
 
         def make_tanh(u):
-            if u < 8:
-                tanh_b[u] = turned_tanh(u, wb_raw[0][:].bitcast(FP4X4), wb_raw_s[:, 0:512], -1.0, "tanh_b", False)
-                tanh_a[u] = turned_tanh(u, wa_w[0][:].bitcast(FP8X4), wa_s[0][:], 1.0, "tanh_a", False)
-            elif u < TURNED:
-                tanh_b[u] = turned_tanh(u, wb_w[:].bitcast(FP4X4), wb_s[:], -1.0, "tanh_b", True)
-                tanh_a[u] = turned_tanh(u, wa_w[1][:].bitcast(FP8X4), wa_s[1][:], 1.0, "tanh_a", True)
+            if u < GROUPS:
+                tanh_b[u] = turned_tanh(u, wb_raw[0][:].bitcast(FP4X4), wb_raw_s[:, 0:BANK], -1.0, "tanh_b")
+                tanh_a[u] = turned_tanh(u, wa_w[0][:].bitcast(FP8X4), wa_s[0][:], 1.0, "tanh_a")
+            elif is_turned(u):
+                tanh_b[u] = turned_tanh(u, wb_dealt[:].bitcast(FP4X4), wb_dealt_s[:], -1.0, "tanh_b")
+                tanh_a[u] = turned_tanh(u, wa_w[1][:].bitcast(FP8X4), wa_s[1][:], 1.0, "tanh_a")
             else:
-                tanh_b[u] = direct_tanh(u, lambda t: wb_w[:, 256 * t : 256 * (t + 1)].bitcast(FP4X4), wb_s, "tanh_b")
+                tanh_b[u] = direct_tanh(u, lambda t: wb_dealt[:, 2 * P * t : 2 * P * (t + 1)].bitcast(FP4X4), wb_dealt_s, "tanh_b")
                 tanh_a[u] = direct_tanh(u, lambda t: wa_w[1][:, P * t : P * (t + 1)].bitcast(FP8X4), wa_s[1], "tanh_a")
 
         def make_factors(u):
-            b = u // 8
-            bank = psum.tile([P, 512], F32, name="f3_bank", tag="late", bufs=2)
-            product(bank, u, lambda t: w3_w[b][:, P * t : P * (t + 1)].bitcast(FP8X4), w3_s[b])
+            b = u // GROUPS
+            f3_bank = psum.tile([P, BANK], F32, name="f3_bank", tag="f3_bank", bufs=2)
+            direct_product(f3_bank, u, lambda t: w3_w[b][:, P * t : P * (t + 1)].bitcast(FP8X4), w3_s[b])
             if u == UNITS - 1:
-                held = keep.tile([P, 512], F32, name="held_last", align_bytes=64)
+                held = keep.tile([P, BANK], F32, name="held_last", align_bytes=64)
             else:
-                held = work.tile([P, 512], F32, name="held", tag="held", bufs=4, align_bytes=64)
-            if u < TURNED:
-                nc.scalar.copy(by_four(held[:]), woven(bank))
-                bank = psum.tile([P, 512], F32, name="diff", tag="diff", bufs=3)
+                held = work.tile([P, BANK], F32, name="held", tag="held", bufs=4, align_bytes=64)
+            if is_turned(u):
+                nc.scalar.copy(by_four(held[:]), woven(f3_bank))
+                diff_bank = psum.tile([P, BANK], F32, name="diff_bank", tag="sums", bufs=3)
                 for t in range(4):
                     cols = slice(P * t, P * (t + 1))
-                    nc.tensor.matmul(bank[:, cols], tanh_a[u][:, cols], ident[:], start=True, stop=False, is_transpose=True)
-                    nc.tensor.matmul(bank[:, cols], tanh_b[u][:, cols], ident[:], start=False, stop=True, is_transpose=True)
+                    nc.tensor.matmul(diff_bank[:, cols], tanh_a[u][:, cols], ident[:], start=True, stop=False, is_transpose=True)
+                    nc.tensor.matmul(diff_bank[:, cols], tanh_b[u][:, cols], ident[:], start=False, stop=True, is_transpose=True)
+                factors[u] = (diff_bank, held)
             else:
                 nc.vector.tensor_tensor(held[:], tanh_a[u][:], tanh_b[u][:], SUB)
-            factors[u] = (bank, held)
+                factors[u] = (f3_bank, held)
 
         def make_h(u):
-            b, j = divmod(u, 8)
+            b, group = divmod(u, GROUPS)
             bank, held = factors[u]
-            nc.vector.tensor_tensor(by_four(h_bf[b][:, 512 * j : 512 * (j + 1)]), woven(bank), by_four(held[:]), MULT)
-
-        def quantize_h(b, lo, hi):
-            quantize(h_w[b][:, lo:hi], h_s[b][:, lo:hi], h_bf[b][:, 4 * lo : 4 * hi])
+            nc.vector.tensor_tensor(by_four(h_bf[b][:, BANK * group : BANK * (group + 1)]), woven(bank), by_four(held[:]), MULT)
 
         def scores(m, lo, hi):
-            bank = psum.tile([P, 512], F32, name="e_bank", tag="diff", bufs=3)
-            half, first = divmod(P * m, 256)
+            e_bank = psum.tile([P, BANK], F32, name="e_bank", tag="sums", bufs=3)
+            half, first = divmod(P * m, HALF)
             for b in range(2):
                 nc.tensor.matmul_mx(
-                    out=bank[:, 0 : hi - lo],
-                    lhsT=v2_w[half][:, 256 * b + first : 256 * b + first + P].bitcast(FP8X4),
+                    out=e_bank[:, 0 : hi - lo],
+                    lhsT=v2_w[half][:, HALF * b + first : HALF * b + first + P].bitcast(FP8X4),
                     lhsT_scale=v2_s[half][4 * b : P, first : first + P],
                     rhs=h_w[b][:, lo:hi].bitcast(FP8X4),
                     rhs_scale=h_s[b][:, lo:hi],
                     start=(b == 0),
                     stop=(b == 1),
                 )
-            nc.scalar.copy(e_t[m][:, lo:hi], bank[:, 0 : hi - lo])
-
-        order = list(range(LEAD))
-        turned = list(range(LEAD, TURNED))
-        for k, u in enumerate(range(TURNED, UNITS)):
-            order.append(u)
-            order.extend(turned[k : k + 1])
-        order.extend(turned[UNITS - TURNED :])
-        h_pieces = {3: (0, 0, 512), 7: (0, 512, 1024), 11: (1, 0, 512), 13: (1, 512, 768), 14: (1, 768, 896), 15: (1, 896, 1024)}
-
-        finished = set()
-        closed = set()
+            nc.scalar.copy(e_t[m][:, lo:hi], e_bank[:, 0 : hi - lo])
 
         def close_piece(u):
-            finished.add(u)
-            for b, lo, hi in h_pieces.values():
-                if (b, lo) not in closed and all(8 * b + j in finished for j in range(lo // P, hi // P)):
-                    closed.add((b, lo))
-                    quantize_h(b, lo, hi)
-                    if b == 1:
-                        scores(0, lo, hi)
-                        scores(1, lo, hi)
+            b, group = divmod(u, GROUPS)
+            width = 2 if u >= UNITS - 4 else 4
+            if (group + 1) % width == 0:
+                lo, hi = P * (group + 1 - width), P * (group + 1)
+                quantize(h_w[b][:, lo:hi], h_s[b][:, lo:hi], h_bf[b][:, 4 * lo : 4 * hi])
+                if b == 1:
+                    scores(0, lo, hi)
 
-        for part in range(3):
-            gather_v_words(part, f"v_w{part}")
-        for part in range(3):
-            gather_v_scales(part, f"v_s{part}")
-        round_plain(nc.scalar.copy, wa_bf[0], wa_head[0], 0)
-        round_plain(nc.scalar.copy, wa_bf[0], wa_head[1], 64)
+        order = list(range(LEAD))
+        for group in range(GROUPS):
+            order.append(GROUPS + group)
+            if LEAD + group < GROUPS:
+                order.append(LEAD + group)
+
+        for lo, hi in zip(EARLY_PATCHES, EARLY_PATCHES[1:]):
+            gather_v(lo, hi, f"v_w{lo}", f"v_s{lo}")
+        for half in range(2):
+            round_in_order(half)
         quantize(wa_w[0][:], wa_s[0][:], wa_bf[0][:])
         for half in range(2):
-            round_weight(nc.vector.tensor_copy, w3_bf[0], w3_head[half][:], 64 * half)
+            round_dealt(w3_bf[0], w3_head[half], HALF // 4 * half)
         for u in order[:AHEAD]:
             make_tanh(u)
         quantize(w3_w[0][:], w3_s[0][:], w3_bf[0][:])
-        gather_v_words(3, "w3_bf0")
-        gather_v_scales(3, "w3_head1")
-        wb_s = keep.tile([P, 512], U8, name="wb_s", tag="w3_head0", align_bytes=64)
-        deal_wb()
+        gather_v(EARLY_PATCHES[-1], S, "w3_bf0", "w3_head1")
+        wb_dealt_s = keep.tile([P, BANK], U8, name="wb_dealt_s", tag="w3_head0", align_bytes=64)
+        nc.vector.tensor_copy(
+            wb_dealt[:].bitcast(U16).rearrange("p (t q) -> p t q", t=4),
+            wb_raw[1][:].bitcast(U16).rearrange("p (q t) -> p t q", t=4),
+        )
+        nc.vector.tensor_copy(
+            wb_dealt_s[:].rearrange("p (t q) -> p t q", t=4),
+            wb_raw_s[:, BANK:H].rearrange("p (q t) -> p t q", t=4),
+        )
 
         for i, u in enumerate(order):
             make_factors(u)
             if i == 0:
-                round_weight(nc.vector.tensor_copy, wa_bf[1], wa_raw[:], 0)
+                round_dealt(wa_bf[1], wa_rest, 0)
             if i == 1:
                 quantize(wa_w[1][:], wa_s[1][:], wa_bf[1][:])
-                round_weight(nc.vector.tensor_copy, w3_bf[1], w3_raw[1][:], 0)
+                round_dealt(w3_bf[1], w3_rest, 0)
             if i + AHEAD < UNITS:
                 make_tanh(order[i + AHEAD])
             if i >= 1:
                 make_h(order[i - 1])
             if i == 2:
                 quantize(w3_w[1][:], w3_s[1][:], w3_bf[1][:])
-            if i == 6:
-                gather_v2(
-                    0,
-                    keep.tile([P, 512], U32, name="v2_w_first", align_bytes=64),
-                    keep.tile([P, 256], U8, name="v2_s_first", align_bytes=64),
-                )
+            if i == PANEL_STEP:
+                gather_v2(0, "v2_w0", "v2_s0")
             if i >= 2:
                 close_piece(order[i - 2])
         make_h(order[-1])
         close_piece(order[-2])
         close_piece(order[-1])
-        gather_v2(
-            1,
-            keep.tile([P, 512], U32, name="v2_w_last", tag="h_bf1", align_bytes=64),
-            keep.tile([P, 256], U8, name="v2_s_last", tag="held_last", align_bytes=64),
-        )
 
-        left = {}
+        gather_v2(1, "h_bf1", "held_last")
+        for m in range(1, S2 // P):
+            for lo in range(0, S, BANK):
+                scores(m, lo, lo + BANK)
 
         def pick_left(m):
-            left[m] = work.tile([P, NP], F32, name="left", tag="left", bufs=2)
+            left[m] = work.tile([P, PAIRS], F32, name="left", tag="left", bufs=2)
             nc.vector.tensor_tensor(left[m][:], e_t[m][:].indirect(pos1_t[:]), leaf_t[:, m, :], ADD)
 
-        for m in range(2, 4):
-            scores(m, 0, 512)
-            scores(m, 512, 1024)
         pick_left(0)
-        for m in range(4):
-            right = work.tile([P, NP], F32, name="right", tag="right", bufs=2)
+        for m in range(S2 // P):
+            right = work.tile([P, PAIRS], F32, name="right", tag="right", bufs=2)
             nc.vector.tensor_copy(right[:], e_t[m][:].indirect(pos2_t[:]))
-            if m + 1 < 4:
+            if m + 1 < S2 // P:
                 pick_left(m + 1)
-            result = work.tile([P, NP], F32, name="result", tag="result", bufs=4)
+            result = work.tile([P, PAIRS], F32, name="result", tag="result", bufs=4)
             nc.vector.scalar_tensor_tensor(result[:], right[:], panel_t[:, m : m + 1], left[m][:], ADD, MULT)
             nc.sync.dma_start(out[P * m : P * (m + 1), :], result[:])

from contextlib import ExitStack

import concourse.mybir as mybir
from concourse.masks import make_identity

K, H, T, S, T3, S2, PAIRS = 512, 1024, 2048, 1024, 1024, 512, 512
FLOPS = 2 * K * H * S * 3 + 2 * H * S2 * S

F32 = mybir.dt.float32
BF16 = mybir.dt.bfloat16
I32 = mybir.dt.int32
U32 = mybir.dt.uint32
U16 = mybir.dt.uint16
U8 = mybir.dt.uint8
FP8X4 = mybir.dt.float8_e4m3fn_x4
FP4X4 = mybir.dt.float4_e2m1fn_x4
ADD = mybir.AluOpType.add
SUB = mybir.AluOpType.subtract
MULT = mybir.AluOpType.mult
TANH = mybir.ActivationFunctionType.Tanh

P = 128
BANK = 512
HALF = 256
GROUPS = S // P
UNITS = 2 * GROUPS
LEAD = 6
AHEAD = 3
MIXED_END = 4
EARLY_PATCHES = (0, 256, 768)
PANEL_STEP = 6


def is_turned(u):
    return u < GROUPS or (u >= UNITS - MIXED_END and u % 2 == 0)


def tile_list_bookmatch_leaf_scores_kernel(
    tc, tab_words, tab_scales, tab2_words, tab2_scales, wa, wb_words, wb_scales, w3, leaf, panel, offs, offs2, pos1, pos2, out
):
    nc = tc.nc
    with ExitStack() as ctx:
        lists = ctx.enter_context(tc.tile_pool(name="lists", bufs=1))
        keep = ctx.enter_context(tc.tile_pool(name="keep", bufs=1))
        work = ctx.enter_context(tc.tile_pool(name="work", bufs=1))
        psum = ctx.enter_context(tc.psum_pool(name="psum", bufs=1))

        offs_t = lists.tile([P, S // 16], U16, name="offs_t")
        offs2_t = lists.tile([P, S2 // 16], U16, name="offs2_t")
        pos1_t = lists.tile([P, PAIRS // 16], U16, name="pos1_t")
        pos2_t = lists.tile([P, PAIRS // 16], U16, name="pos2_t")

        tab_w = keep.tile([P, T], I32, name="tab_w", align_bytes=64)
        tab_s = keep.tile([P, T], U8, name="tab_s", align_bytes=64)
        tab2_w = [keep.tile([P, T3], I32, name=f"tab2_w{b}", align_bytes=64) for b in range(2)]
        tab2_s = keep.tile([P, T3], U8, name="tab2_s", align_bytes=64)
        wb_raw = [keep.tile([P, 2 * BANK], U8, name=f"wb_raw{b}", align_bytes=64) for b in range(2)]
        wb_raw_s = keep.tile([P, H], U8, name="wb_raw_s", align_bytes=64)
        wa_head = [keep.tile([P, 4, HALF], F32, name=f"wa_head{half}", align_bytes=64) for half in range(2)]
        wa_rest = keep.tile([P, 4, BANK], F32, name="wa_rest", align_bytes=64)
        w3_head = [keep.tile([P, 4, HALF], F32, name=f"w3_head{half}", align_bytes=64) for half in range(2)]
        w3_rest = keep.tile([P, 4, BANK], F32, name="w3_rest", align_bytes=64)
        leaf_t = keep.tile([P, 4, PAIRS], F32, name="leaf_t", align_bytes=64)
        panel_t = keep.tile([P, 4], F32, name="panel_t", align_bytes=64)

        nc.gpsimd.memset(tab_s[:].bitcast(I32), 0)
        nc.gpsimd.memset(wb_raw_s[:].bitcast(I32), 0)
        nc.vector.memset(tab2_s[:].bitcast(I32), 0)

        wa_rows = wa.rearrange("(p i) c -> p i c", i=4)
        w3_rows = w3.rearrange("(p i) c -> p i c", i=4)
        nc.sync.dma_start(offs_t[:], offs)
        nc.sync.dma_start(tab_w[:], tab_words[0].rearrange("p c i -> p (c i)").bitcast(I32))
        for quad in range(4):
            rows = tab_scales[0, 4 * quad : 4 * quad + 4, :]
            nc.sync.dma_start(tab_s[32 * quad : 32 * quad + 4, :].bitcast(I32), rows.bitcast(I32))
        for half in range(2):
            nc.sync.dma_start(wa_head[half][:], wa_rows[:, :, HALF * half : HALF * (half + 1)])
        nc.sync.dma_start(wb_raw[0][:].bitcast(I32), wb_words[0, :, 0 : 2 * BANK].bitcast(I32))
        for quad in range(4):
            rows = wb_scales[0, 4 * quad : 4 * quad + 4, :]
            nc.sync.dma_start(wb_raw_s[32 * quad : 32 * quad + 4, :].bitcast(I32), rows.bitcast(I32))
        for half in range(2):
            nc.sync.dma_start(w3_head[half][:], w3_rows[:, :, HALF * half : HALF * (half + 1)])
        nc.sync.dma_start(wb_raw[1][:].bitcast(I32), wb_words[0, :, 2 * BANK : 4 * BANK].bitcast(I32))
        nc.sync.dma_start(wa_rest[:], wa_rows[:, :, BANK:H])
        nc.sync.dma_start(w3_rest[:], w3_rows[:, :, BANK:H])
        nc.sync.dma_start(offs2_t[:], offs2)
        for b in range(2):
            nc.sync.dma_start(tab2_w[b][:], tab2_words[b].rearrange("p c i -> p (c i)").bitcast(I32))
        for quad in range(4):
            rows = tab2_scales[:, 4 * quad : 4 * quad + 4, :]
            nc.sync.dma_start(tab2_s[32 * quad : 32 * quad + 8, :].bitcast(I32), rows.bitcast(I32))
        nc.sync.dma_start(pos1_t[:], pos1)
        nc.sync.dma_start(pos2_t[:], pos2)
        with nc.allow_non_contiguous_dma(reason="one panel value a partition"):
            nc.sync.dma_start(panel_t[:], panel.rearrange("(m p) -> p m", p=P))
        nc.sync.dma_start(leaf_t[:], leaf.rearrange("(m p) n -> p m n", p=P))

        wb_dealt = keep.tile([P, 2 * BANK], U8, name="wb_dealt", align_bytes=64)
        ident = keep.tile([P, P], F32, name="ident", align_bytes=64)
        nc.vector.memset(ident[:], 0.0)
        make_identity(nc, ident[:], nomemset=True)
        wa_bf = [keep.tile([P, 4 * BANK], BF16, name=f"wa_bf{b}", align_bytes=64) for b in range(2)]
        w3_bf = [keep.tile([P, 4 * BANK], BF16, name=f"w3_bf{b}", align_bytes=64) for b in range(2)]
        wa_w = [keep.tile([P, BANK], U32, name=f"wa_w{b}", align_bytes=64) for b in range(2)]
        wa_s = [keep.tile([P, BANK], U8, name=f"wa_s{b}", align_bytes=64) for b in range(2)]
        w3_w = [keep.tile([P, BANK], U32, name=f"w3_w{b}", align_bytes=64) for b in range(2)]
        w3_s = [keep.tile([P, BANK], U8, name=f"w3_s{b}", align_bytes=64) for b in range(2)]
        h_bf = [keep.tile([P, 4 * S], BF16, name=f"h_bf{b}", align_bytes=64) for b in range(2)]
        h_w = [keep.tile([P, S], U32, name=f"h_w{b}", align_bytes=64) for b in range(2)]
        h_s = [keep.tile([P, S], U8, name=f"h_s{b}", align_bytes=64) for b in range(2)]
        e_t = [keep.tile([P, S], F32, name=f"e{m}", align_bytes=64) for m in range(S2 // P)]

        patch_groups = []
        v2_w, v2_s = {}, {}
        tanh_a, tanh_b, factors, left = {}, {}, {}, {}

        def gather_v(lo, hi, words_tag, scales_tag):
            picks = offs_t[:, lo // 16 : hi // 16]
            words = keep.tile([P, hi - lo], U32, name=f"v_w{lo}", tag=words_tag, align_bytes=64)
            scales = keep.tile([P, hi - lo], U8, name=f"v_s{lo}", tag=scales_tag, align_bytes=64)
            nc.vector.tensor_copy(words[:], tab_w[:].bitcast(U32).indirect(picks))
            nc.vector.tensor_copy(scales[:], tab_s[:].indirect(picks))
            for first in range(0, hi - lo, P):
                patch_groups.append((words[:, first : first + P].bitcast(FP8X4), scales[:, first : first + P]))

        def gather_v2(half, words_tag, scales_tag):
            picks = offs2_t[:, HALF * half // 16 : HALF * (half + 1) // 16]
            v2_w[half] = keep.tile([P, 2 * HALF], U32, name=f"v2_w{half}", tag=words_tag, align_bytes=64)
            v2_s[half] = keep.tile([P, HALF], U8, name=f"v2_s{half}", tag=scales_tag, align_bytes=64)
            for b in range(2):
                nc.vector.tensor_copy(v2_w[half][:, HALF * b : HALF * (b + 1)], tab2_w[b][:].bitcast(U32).indirect(picks))
            nc.vector.tensor_copy(v2_s[half][:], tab2_s[:].indirect(picks))

        def round_in_order(half):
            quads = slice(HALF // 4 * half, HALF // 4 * (half + 1))
            nc.scalar.copy(
                wa_bf[0][:].rearrange("p (q t i) -> p q i t", t=4, i=4)[:, quads],
                wa_head[half][:].rearrange("p i (q t) -> p q i t", t=4),
            )

        def round_dealt(rounded, raw, q0):
            count = raw.shape[2] // 4
            nc.vector.tensor_copy(
                rounded[:].rearrange("p (t q i) -> p q i t", t=4, i=4)[:, q0 : q0 + count],
                raw[:].rearrange("p i (q t) -> p q i t", t=4),
            )

        def quantize(words, scales, rounded):
            nc.vector.quantize_mx(out=words.bitcast(FP8X4), scales=scales, in_=rounded)

        def direct_product(bank, u, weight_words, weight_scales):
            v_words, v_scales = patch_groups[u % GROUPS]
            for t in range(4):
                nc.tensor.matmul_mx(
                    out=bank[:, P * t : P * (t + 1)],
                    lhsT=weight_words(t),
                    lhsT_scale=weight_scales[:, P * t : P * (t + 1)],
                    rhs=v_words,
                    rhs_scale=v_scales,
                    start=True,
                    stop=True,
                )

        def woven(bank):
            return bank[:].rearrange("p (t j) -> p j t", t=4)

        def by_four(ap):
            return ap.rearrange("p (j t) -> p j t", t=4)

        def turned_tanh(u, words, scales, sign, name):
            v_words, v_scales = patch_groups[u % GROUPS]
            bank = psum.tile([P, BANK], F32, name="pre_tanh", tag="pre_tanh", bufs=3)
            nc.tensor.matmul_mx(
                out=bank[:], lhsT=v_words, lhsT_scale=v_scales, rhs=words, rhs_scale=scales, start=True, stop=True
            )
            result = work.tile([P, BANK], F32, name=name, tag=name, bufs=6, align_bytes=64)
            pattern = "p (q t) -> p t q" if u < GROUPS else "p (t q) -> p t q"
            nc.scalar.activation(result[:].rearrange("p (t q) -> p t q", t=4), bank[:].rearrange(pattern, t=4), TANH, scale=sign)
            return result

        def direct_tanh(u, weight_words, weight_scales, name):
            bank = psum.tile([P, BANK], F32, name="pre_tanh", tag="pre_tanh", bufs=3)
            direct_product(bank, u, weight_words, weight_scales)
            result = work.tile([P, BANK], F32, name=name, tag=name, bufs=6, align_bytes=64)
            nc.scalar.activation(by_four(result[:]), woven(bank), TANH)
            return result

        def make_tanh(u):
            if u < GROUPS:
                tanh_b[u] = turned_tanh(u, wb_raw[0][:].bitcast(FP4X4), wb_raw_s[:, 0:BANK], -1.0, "tanh_b")
                tanh_a[u] = turned_tanh(u, wa_w[0][:].bitcast(FP8X4), wa_s[0][:], 1.0, "tanh_a")
            elif is_turned(u):
                tanh_b[u] = turned_tanh(u, wb_dealt[:].bitcast(FP4X4), wb_dealt_s[:], -1.0, "tanh_b")
                tanh_a[u] = turned_tanh(u, wa_w[1][:].bitcast(FP8X4), wa_s[1][:], 1.0, "tanh_a")
            else:
                tanh_b[u] = direct_tanh(u, lambda t: wb_dealt[:, 2 * P * t : 2 * P * (t + 1)].bitcast(FP4X4), wb_dealt_s, "tanh_b")
                tanh_a[u] = direct_tanh(u, lambda t: wa_w[1][:, P * t : P * (t + 1)].bitcast(FP8X4), wa_s[1], "tanh_a")

        def make_factors(u):
            b = u // GROUPS
            f3_bank = psum.tile([P, BANK], F32, name="f3_bank", tag="f3_bank", bufs=2)
            direct_product(f3_bank, u, lambda t: w3_w[b][:, P * t : P * (t + 1)].bitcast(FP8X4), w3_s[b])
            if u == UNITS - 1:
                held = keep.tile([P, BANK], F32, name="held_last", align_bytes=64)
            else:
                held = work.tile([P, BANK], F32, name="held", tag="held", bufs=4, align_bytes=64)
            if is_turned(u):
                nc.scalar.copy(by_four(held[:]), woven(f3_bank))
                diff_bank = psum.tile([P, BANK], F32, name="diff_bank", tag="sums", bufs=3)
                for t in range(4):
                    cols = slice(P * t, P * (t + 1))
                    nc.tensor.matmul(diff_bank[:, cols], tanh_a[u][:, cols], ident[:], start=True, stop=False, is_transpose=True)
                    nc.tensor.matmul(diff_bank[:, cols], tanh_b[u][:, cols], ident[:], start=False, stop=True, is_transpose=True)
                factors[u] = (diff_bank, held)
            else:
                nc.vector.tensor_tensor(held[:], tanh_a[u][:], tanh_b[u][:], SUB)
                factors[u] = (f3_bank, held)

        def make_h(u):
            b, group = divmod(u, GROUPS)
            bank, held = factors[u]
            nc.vector.tensor_tensor(by_four(h_bf[b][:, BANK * group : BANK * (group + 1)]), woven(bank), by_four(held[:]), MULT)

        def scores(m, lo, hi):
            e_bank = psum.tile([P, BANK], F32, name="e_bank", tag="sums", bufs=3)
            half, first = divmod(P * m, HALF)
            for b in range(2):
                nc.tensor.matmul_mx(
                    out=e_bank[:, 0 : hi - lo],
                    lhsT=v2_w[half][:, HALF * b + first : HALF * b + first + P].bitcast(FP8X4),
                    lhsT_scale=v2_s[half][4 * b : P, first : first + P],
                    rhs=h_w[b][:, lo:hi].bitcast(FP8X4),
                    rhs_scale=h_s[b][:, lo:hi],
                    start=(b == 0),
                    stop=(b == 1),
                )
            nc.scalar.copy(e_t[m][:, lo:hi], e_bank[:, 0 : hi - lo])

        def close_piece(u):
            b, group = divmod(u, GROUPS)
            width = 2 if u >= UNITS - 4 else 4
            if (group + 1) % width == 0:
                lo, hi = P * (group + 1 - width), P * (group + 1)
                quantize(h_w[b][:, lo:hi], h_s[b][:, lo:hi], h_bf[b][:, 4 * lo : 4 * hi])
                if b == 1:
                    scores(0, lo, hi)

        order = list(range(LEAD))
        for group in range(GROUPS):
            order.append(GROUPS + group)
            if LEAD + group < GROUPS:
                order.append(LEAD + group)

        for lo, hi in zip(EARLY_PATCHES, EARLY_PATCHES[1:]):
            gather_v(lo, hi, f"v_w{lo}", f"v_s{lo}")
        for half in range(2):
            round_in_order(half)
        quantize(wa_w[0][:], wa_s[0][:], wa_bf[0][:])
        for half in range(2):
            round_dealt(w3_bf[0], w3_head[half], HALF // 4 * half)
        for u in order[:AHEAD]:
            make_tanh(u)
        quantize(w3_w[0][:], w3_s[0][:], w3_bf[0][:])
        gather_v(EARLY_PATCHES[-1], S, "w3_bf0", "w3_head1")
        wb_dealt_s = keep.tile([P, BANK], U8, name="wb_dealt_s", tag="w3_head0", align_bytes=64)
        nc.vector.tensor_copy(
            wb_dealt[:].bitcast(U16).rearrange("p (t q) -> p t q", t=4),
            wb_raw[1][:].bitcast(U16).rearrange("p (q t) -> p t q", t=4),
        )
        nc.vector.tensor_copy(
            wb_dealt_s[:].rearrange("p (t q) -> p t q", t=4),
            wb_raw_s[:, BANK:H].rearrange("p (q t) -> p t q", t=4),
        )

        for i, u in enumerate(order):
            make_factors(u)
            if i == 0:
                round_dealt(wa_bf[1], wa_rest, 0)
            if i == 1:
                quantize(wa_w[1][:], wa_s[1][:], wa_bf[1][:])
                round_dealt(w3_bf[1], w3_rest, 0)
            if i + AHEAD < UNITS:
                make_tanh(order[i + AHEAD])
            if i >= 1:
                make_h(order[i - 1])
            if i == 2:
                quantize(w3_w[1][:], w3_s[1][:], w3_bf[1][:])
            if i == PANEL_STEP:
                gather_v2(0, "v2_w0", "v2_s0")
            if i >= 2:
                close_piece(order[i - 2])
        make_h(order[-1])
        close_piece(order[-2])
        close_piece(order[-1])

        gather_v2(1, "h_bf1", "held_last")
        for m in range(1, S2 // P):
            for lo in range(0, S, BANK):
                scores(m, lo, lo + BANK)

        def pick_left(m):
            left[m] = work.tile([P, PAIRS], F32, name="left", tag="left", bufs=2)
            nc.vector.tensor_tensor(left[m][:], e_t[m][:].indirect(pos1_t[:]), leaf_t[:, m, :], ADD)

        pick_left(0)
        for m in range(S2 // P):
            right = work.tile([P, PAIRS], F32, name="right", tag="right", bufs=2)
            nc.vector.tensor_copy(right[:], e_t[m][:].indirect(pos2_t[:]))
            if m + 1 < S2 // P:
                pick_left(m + 1)
            result = work.tile([P, PAIRS], F32, name="result", tag="result", bufs=4)
            nc.vector.scalar_tensor_tensor(result[:], right[:], panel_t[:, m : m + 1], left[m][:], ADD, MULT)
            nc.sync.dma_start(out[P * m : P * (m + 1), :], result[:])
